import numpy as np, ml_dtypes
CORES = [2,6,10,14,18,22,26,30]
N = 8
BF = ml_dtypes.bfloat16
B, S, D, SH = 1, 2048, 8192, 4
W, BC = N * B, 32
LAST = (2 * 255 * 255) >> SH
def middle(m):
    return 16 * (m % 16) + 8, 16 * (m // 16) + 8
def index(p, x, y):
    return ((x - int(p[0])) ** 2 + (y - int(p[1])) ** 2) >> SH
def loud(d, rng, cells):
    t = rng.integers(0, S, (N, 8)); sg = rng.choice(np.array([-15.0, 15.0]), 16); v = d["tr"].reshape(N, 8, 16, S); x, y = middle(np.array(cells))
    ld = sg - np.sign(sg) * rng.integers(0, 2, (N, 8, 16))
    for q in range(N):
        for g in range(8):
            d["tau"][q, g, index(d["pos"][q, g], x, y)] = t[q, g]; v[q, g, :, t[q, g]] = ld[q, g].astype(BF)
    return t, ld
def setup_inputs(rng):
    tr = rng.integers(-15, 16, (N, 128, S), dtype=np.int8).astype(np.float32).astype(BF)
    pos = rng.integers(0, 256, (N, 8, 2)).astype(np.int32)
    t = np.floor(np.sqrt(np.arange(D) / D) * (rng.random((N, 8, 1)) * 0.5 + 0.25) * S).astype(np.int64) + rng.integers(0, S // 4, (N, 8, D))
    return {"tr": tr, "pos": pos, "tau": t.astype(np.int32)}
def setup_inputs_ends(rng):
    d = setup_inputs(rng); c = np.array([[0, 0], [0, 255], [255, 0], [255, 255]])
    d["pos"] = np.stack([c[rng.permutation(8) % 4] for q in range(N)]).astype(np.int32)
    t = rng.integers(0, S, (N, 8, D)); t[:, :, 0] = 0; t[:, :, LAST] = S - 1; d["tau"] = t.astype(np.int32)
    e = rng.integers(0, 2, W); e[0] = 0; e[W - 1] = 1
    loud(d, rng, np.arange(W) * BC + e * (BC - 1)); return d
def setup_inputs_ties(rng):
    d = setup_inputs(rng); s = int(rng.integers(0, 3)); cells = []
    for k in range(W):
        z = (k + s) % 3; o = [0, BC - 1] if z == 0 else rng.choice(BC, 2, replace=False) if z == 1 else range(BC)
        cells += [k * BC + int(i) for i in o]
    loud(d, rng, cells); return d
def setup_inputs_close(rng):
    d = setup_inputs(rng); k = np.arange(W); lo = k * BC + rng.integers(0, BC // 2, W); hi = k * BC + BC // 2 + rng.integers(0, BC // 2, W); x, y = middle(lo)
    d["pos"][k % N, k // N, 0] = x; d["pos"][k % N, k // N, 1] = y
    t, ld = loud(d, rng, np.concatenate([lo, hi])); v = d["tr"].reshape(N, 8, 16, S); m = np.abs(np.sum(ld, axis=(0, 1)))
    for i in range(W):
        q, g = i % N, i // N; u = (int(t[q, g]) + int(rng.integers(1, S))) % S; h = ld[q, g].copy(); s = int(rng.integers(0, 16))
        if i % 2:
            z = [(m[a] - m[b], a, b) for a in range(16) for b in range(16) if m[a] > m[b] + 1 and abs(h[b]) < 15]
            if z:
                s, b = min(z)[1:]; h[b] = h[b] + np.sign(h[b])
        h[s] = h[s] - np.sign(h[s])
        d["tau"][q, g, 0] = u; v[q, g, :, u] = h.astype(BF)
    return d
def setup_inputs_steps(rng):
    d = setup_inputs(rng); d["pos"] = np.repeat(rng.integers(0, 256, (N, 1, 2)), 8, axis=1).astype(np.int32)
    d["tau"] = np.repeat(rng.integers(0, S, (N, 8, D // 64)), 64, axis=2).astype(np.int32); return d
def setup_inputs_spread(rng):
    d = setup_inputs(rng); a = rng.choice(np.array([0, 1, 4, 15], np.int8), (N, 8, 1, S))
    v = np.clip(rng.integers(-15, 16, (N, 8, 16, S), dtype=np.int8), -a, a)
    d["tr"] = v.reshape(N, 128, S).astype(np.float32).astype(BF)
    d["pos"] = np.floor(256 * rng.random((N, 8, 2)) ** 3).astype(np.int32); d["tau"] = np.floor(S * rng.random((N, 8, D)) ** 3).astype(np.int32); return d
def check_inputs(d):
    bad = []; v = np.asarray(d["tr"]).astype(np.float32)
    if not ((np.abs(v) <= 15) & (np.rint(v) == v)).all(): bad.append("samples")
    if not ((d["pos"] >= 0) & (d["pos"] <= 255)).all(): bad.append("places")
    if not ((d["tau"] >= 0) & (d["tau"] < S)).all(): bad.append("times")
    return bad
def focus(v, pos, tau, x, y):
    a = np.zeros((16, len(x)), np.int64)
    for q in range(N):
        for g in range(8): a += v[q, g][:, tau[q, g][index(pos[q, g], x, y)]]
    return a
def reference(tr, pos, tau):
    v = tr.astype(np.float32).astype(np.int32).reshape(N, 8, 16, S)
    x, y = middle(np.arange(256)); c = focus(v, pos, tau, x, y)
    e = np.sum(c * c, axis=0).reshape(W, BC)
    w = np.arange(W) * BC + np.argmax(e, axis=1)
    j = np.arange(256); x = (16 * (w % 16)[:, None] + j % 16).reshape(-1); y = (16 * (w // 16)[:, None] + j // 16).reshape(-1)
    fine = focus(v, pos, tau, x, y).reshape(16, N, B * 256).transpose(1, 0, 2)
    return {"y": np.ascontiguousarray(fine).astype(np.float32), "w": np.tile(w.reshape(1, 1, W), (N, 1, 1)).astype(np.float32)}

@@ -1,0 +1,358 @@
+from concourse.bass import DstId, RemoteDMATransfer
+from concourse.mybir import AluOpType, AxisListType, ActivationFunctionType
+
+ZC = 510
+ZL = 16 * ZC
+A1, A2 = 240, 288
+
+F32, B16, H16, I32, U16 = "float32", "bfloat16", "float16", "int32", "uint16"
+SCRATCH = {
+    "pin": ("sbuf", [128, 8, 64], I32), "pf": ("sbuf", [128, 4, 8, 16], H16),
+    "posi": ("sbuf", [8, 2], I32), "posb": ("sbuf", [8, 2], B16), "posf": ("sbuf", [8, 2], F32),
+    "feat": ("sbuf", [8, 128], B16), "gsel": ("sbuf", [8, 128], F32), "sel8": ("sbuf", [8, 128], B16),
+    "rrow": ("sbuf", [1, 128], B16), "trow": ("sbuf", [1, 128], B16),
+    "kw": ("sbuf", [1, 8], F32), "wout": ("sbuf", [1, 8], F32),
+}
+for _nm, _w, _t in [
+        ("trs", 2048, B16), ("nat", 512, F32), ("off", 512, U16), ("zed", ZL, B16), ("ints", 4, I32), ("cols", 4, F32),
+        ("colg", 1, F32), ("col8", 1, F32), ("cu", 144, F32), ("cm8", 128, F32), ("aj", 256, F32), ("bj", 256, F32),
+        ("qg", 144, H16), ("qs", 144, B16), ("idb", 128, B16), ("idh", 128, H16), ("idf", 128, F32), ("em", 128, F32),
+        ("zero", 32, F32), ("dfw", 32, F32), ("kcol", 128, F32), ("kmask", 128, F32), ("coef", 128, F32),
+        ("gee", 128, B16), ("kyi", 128, F32), ("kysq", 128, F32), ("cst", 128, F32), ("lh4", 128, B16), ("lhw", 1, B16),
+        ("neg", 2, F32), ("b8", 2, F32), ("b8s", 2, F32), ("xx", 256, F32), ("yy", 256, F32), ("ss", 256, I32),
+        ("rj", 256, I32), ("mask", 256, F32), ("dxc", 1, F32), ("rx2", 1, F32), ("dyc", 16, F32), ("cidx", 16, U16),
+        ("yg", 256, H16), ("off2", 16, U16), ("cg", 256, B16), ("sendc", 32, B16), ("landc", 256, B16), ("sq", 32, F32),
+        ("cmx", 32, F32), ("uu", 32, F32), ("ud", 32, F32), ("ff", 1, F32), ("rhs", 128, B16), ("lst", 128, U16),
+        ("fg", 2048, B16), ("sendf", 256, B16), ("landf", 256, B16), ("yout", 32, F32)]:
+    SCRATCH[_nm] = ("sbuf", [128, _w], _t)
+for _nm in ["pt", "po", "pc", "pe", "ps", "pf0", "pf1", "pm"]:
+    SCRATCH[_nm] = ("psum", [128, 512], F32)
+SEMAPHORES = ["s_pos", "s_tau", "s_tr", "s_w", "s_y",
+              "i_p", "i_sel", "i_aj", "i_bj", "i_u", "i_m8", "i_d", "i_k", "i_c", "i_ky", "i_rr", "i_kw",
+              "m_z", "m_d0", "m_d1", "m_co", "m_lw0", "m_lw1", "m_ft", "m_tr0", "m_tr1",
+              "v_int", "v_col", "v_c2", "v_sel", "v_qg", "v_qs", "v_id", "v_idh", "v_em", "v_km", "v_g", "v_posb",
+              "v_posf", "v_neg", "v_feat", "v_cidx", "v_ss", "v_rj", "v_mask", "v_pf", "v_yg", "v_off", "v_off2", "v_cg",
+              "v_sendc", "v_lh4", "v_z", "v_cm", "v_u", "v_ud", "v_f", "v_rhs", "v_l0", "v_l1", "v_g0", "v_g1", "v_e0",
+              "v_e1", "v_w", "v_y",
+              "a_xx", "a_dc", "a_rx", "a_ky", "a_cst", "a_n", "a_cg", "a_z", "a_sq", "a_g0", "a_g1",
+              "t_pos", "t_t", "t_off", "t_c", "t_lh4", "t_sum", "t_e", "t_s", "t_w", "t_f0", "t_f1", "t_y",
+              "r_c", "r_f0", "r_f1", "l_c", "l_f"]
+
+
+def rank_program(g, core, T, topo):
+    rank = T.rank_of(core)
+    if rank is None:
+        return
+    A, F = AluOpType, ActivationFunctionType
+    cores = list(T.cores)
+    n = len(cores)
+    half = n // 2
+    V, S, E, Y = g.vector, g.scalar, g.tensor, g.sync
+    Q = {"g": g, "v": V, "s": S, "t": E, "y": Y}
+    cnt, seen = {}, {}
+
+    def fin(ins, name, k=1):
+        ins.then_inc(T.sem[name], k)
+        cnt[name] = cnt.get(name, 0) + k
+
+    def need(q, *names):
+        for nm in names:
+            if seen.get((q, nm), 0) < cnt[nm]:
+                Q[q].wait_ge(T.sem[nm], cnt[nm])
+                seen[(q, nm)] = cnt[nm]
+
+    def order(r):
+        h = r // half
+        return [k for hh in (1 - h, h) for k in range(half * hh, half * hh + half)]
+
+    def bits(es):
+        return sum(1 << e for e in es)
+
+    def masks(r, dests):
+        src = cores[r]
+        off = [d for d in dests if topo.chip(cores[d]) != topo.chip(src)]
+        out, taken = {}, []
+        for i, d in enumerate(off):
+            es = topo.engines(src, cores[d])
+            w = len(es) // len(off)
+            out[d] = es[i * w:i * w + w]
+            taken = es
+        for d in dests:
+            if d not in off:
+                out[d] = [e for e in topo.engines(src, cores[d]) if e not in taken][:2]
+        return out
+
+    def halves(r):
+        o = order(r)
+        return [d for d in o[:half] if d != r], [d for d in o[half:] if d != r]
+
+    def coarse_masks(r):
+        src = cores[r]
+        off = [d for d in range(n) if topo.chip(cores[d]) != topo.chip(src)]
+        on = [d for d in range(n) if d != r and d not in off]
+        oe = topo.engines(src, cores[off[0]])
+        ne = [e for e in topo.engines(src, cores[on[0]]) if e not in oe][:2] if on else []
+        return off, oe, on, ne
+
+    def dst(d):
+        rid, pid, _ = topo.addr(cores[d])
+        return DstId(rid=rid, pnc=pid)
+
+    korder = order(rank)
+
+    fin(Y.dma_start(T.posi[:], T.pos[:]), "s_pos", 16)
+    for s in range(8):
+        q = Y if s < 4 else S
+        fin(q.dma_start(T.pin[:, s, :], T.tau[s:s + 1, :]), "s_tau", 16)
+    fin(Y.dma_start(T.trs[0:64, :], T.tr[0:64, :]), "s_tr", 16)
+    fin(S.dma_start(T.trs[64:128, :], T.tr[64:128, :]), "s_tr", 16)
+
+    def iota(ap, pat, base, cm, name):
+        fin(g.iota(ap, pat, base, cm, allow_small_or_imprecise_dtypes=True), name)
+
+    fin(g.iota(T.ints[:, 0:1], [[1, 1]], 0, 1), "i_p")
+    iota(T.gsel[:], [[1, 8], [0, 16]], 0, -1, "i_sel")
+    iota(T.aj[:], [[0, 16], [1, 16]], 0, 0, "i_aj")
+    iota(T.bj[:], [[1, 16], [0, 16]], 0, 0, "i_bj")
+    iota(T.cu[:], [[1, 144]], 0, 0, "i_u")
+    iota(T.cm8[:], [[0, 16], [1, 8]], 0, 0, "i_m8")
+    for h in range(2):
+        k0 = korder[half * h]
+        c = slice(64 * h, 64 * h + 64)
+        iota(T.kcol[:, c], [[0, 8], [1, 4], [0, 2]], k0, 0, "i_k")
+        iota(T.coef[:, c], [[16, 8], [256, 4], [8, 2]], 64 + 256 * k0, 0, "i_c")
+        iota(T.kyi[:, c], [[2, 8], [32, 4], [1, 2]], 32 * k0, 0, "i_ky")
+    iota(T.dfw[0:32, :], [[0, 2], [2, 16]], 1, 0, "i_d")
+    iota(T.rrow[:], [[0, 8], [1, 16]], 0, 0, "i_rr")
+    iota(T.kw[:], [[32, 8]], 0, 0, "i_kw")
+
+    def ms(ap, x, name):
+        fin(V.memset(ap, x), name)
+
+    ms(T.zero[:], 0.0, "m_z")
+    ms(T.dfw[32:64, :], 1.0, "m_d0")
+    ms(T.dfw[64:128, :], 0.0, "m_d0")
+    ms(T.lhw[:], 0.0, "m_lw0")
+    ms(T.feat[:], 1.0, "m_ft")
+    ms(T.trow[:], 0.0, "m_tr0")
+    need("v", "m_d0", "m_lw0", "m_tr0")
+    ms(T.dfw[32:64, 15:16], -15.0, "m_d1")
+    ms(T.dfw[64:128, 15:16], 1.0, "m_d1")
+    ms(T.lhw[32:64, :], 1.0 / 32, "m_lw1")
+    ms(T.lhw[96:128, :], 0.5, "m_lw1")
+    ms(T.trow[:, 32:64], 1.0, "m_tr1")
+    need("v", "i_p")
+    fin(V.tensor_scalar(T.ints[:, 1:2], T.ints[:, 0:1], 15, None, A.bitwise_and), "v_int")
+    fin(V.tensor_scalar(T.ints[:, 2:3], T.ints[:, 0:1], 7, None, A.bitwise_and), "v_int")
+    fin(V.tensor_scalar(T.ints[:, 3:4], T.ints[:, 0:1], 112, None, A.bitwise_and), "v_int")
+    need("v", "v_int")
+    fin(V.tensor_copy(T.cols[:], T.ints[:]), "v_col")
+    need("v", "v_col")
+    fin(V.tensor_scalar(T.colg[:], T.cols[:, 3:4], 15.0, None, A.add), "v_c2")
+    fin(V.tensor_scalar(T.col8[:], T.cols[:, 1:2], 8.0, 7.0, A.mult, A.add), "v_c2")
+    need("v", "i_sel")
+    fin(V.tensor_scalar(T.sel8[:], T.gsel[:], 0.0, None, A.is_equal), "v_sel")
+    need("v", "s_pos")
+    fin(V.tensor_copy(T.posb[:], T.posi[:]), "v_posb")
+    need("t", "v_sel", "v_posb")
+    fin(E.matmul(T.pm[:, 0:2], T.sel8[:], T.posb[:], True, True), "t_pos")
+    need("v", "v_c2", "i_u")
+    fin(V.tensor_scalar(T.idh[:], T.cu[:, 0:128], T.cols[:, 0:1], None, A.is_equal), "v_idh")
+    need("v", "t_pos")
+    fin(V.tensor_scalar(T.b8[:], T.pm[:, 0:2], -1.0, 8.0, A.mult, A.add), "v_neg")
+    fin(V.tensor_scalar(T.b8s[:], T.pm[:, 0:2], -0.0625, 0.5, A.mult, A.add), "v_neg")
+    fin(V.tensor_scalar(T.neg[:], T.pm[:, 0:2], -1.0, None, A.mult), "v_neg")
+    need("s", "v_neg", "i_aj", "i_bj", "v_col", "i_u")
+    fin(S.activation(T.dyc[:], T.cu[:, 0:16], F.Square, bias=T.b8s[:, 1:2]), "a_dc")
+    fin(S.activation(T.dxc[:], T.cols[:, 1:2], F.Square, bias=T.b8s[:, 0:1]), "a_dc")
+    fin(S.activation(T.xx[:], T.aj[:], F.Square, bias=T.b8[:, 0:1], scale=16.0), "a_xx")
+    fin(S.activation(T.yy[:], T.bj[:], F.Square, bias=T.b8[:, 1:2], scale=16.0), "a_xx")
+    fin(S.activation(T.rx2[:], T.cols[:, 1:2], F.Square, bias=T.neg[:, 0:1]), "a_rx")
+    need("s", "i_ky")
+    fin(S.activation(T.kysq[:], T.kyi[:], F.Square, bias=T.neg[:, 1:2]), "a_ky")
+    need("s", "a_rx", "a_ky")
+    fin(S.activation(T.cst[:], T.kysq[:], F.Identity, bias=T.rx2[:, 0:1]), "a_cst")
+    fin(V.tensor_scalar(T.qg[:], T.cu[:], T.colg[:, 0:1], None, A.is_equal), "v_qg")
+    need("v", "a_dc")
+    fin(V.tensor_scalar(T.cidx[:], T.dyc[:], T.dxc[:, 0:1], -255.0 / 512, A.add, A.add), "v_cidx")
+    need("v", "a_xx")
+    fin(V.tensor_tensor(T.ss[:], T.xx[:], T.yy[:], A.add), "v_ss")
+    need("v", "v_ss")
+    fin(V.tensor_scalar(T.rj[:], T.ss[:], 4, 15, A.arith_shift_right, A.bitwise_and), "v_rj")
+    need("v", "v_rj")
+    fin(V.tensor_scalar(T.mask[:], T.rj[:], T.cols[:, 1:2], None, A.is_equal), "v_mask")
+
+    need("v", "s_tau")
+    for cb in range(4):
+        fin(V.tensor_copy(T.pf[:, cb, :, :], T.pin[:, :, 16 * cb:16 * cb + 16]), "v_pf")
+    need("t", "v_pf", "v_idh")
+    for cb in range(4):
+        fin(E.matmul(T.pt[:, cb::4], T.pf[:, cb, :, :], T.idh[:], True, True), "t_t")
+    need("s", "t_t")
+    fin(S.activation(T.nat[:], T.pt[:], F.Copy), "a_n")
+    fin(V.tensor_scalar(T.qs[:], T.cu[:], T.col8[:, 0:1], None, A.is_equal), "v_qs")
+    need("v", "a_n", "v_cidx", "v_mask")
+    fin(V.tensor_tensor(T.yg[:], T.nat[:, 0:512].indirect(T.cidx[:, 0:16]), T.mask[:], A.mult), "v_yg")
+    need("t", "v_yg", "v_qg")
+    for r in range(16):
+        ins = E.matmul(T.po[:, 0:16], T.qg[:, 15 - r:143 - r], T.yg[:, r::16], r == 0, r == 15)
+        if r == 15:
+            fin(ins, "t_off")
+    fin(V.tensor_copy(T.off[:], T.nat[:]), "v_off")
+    need("v", "t_off")
+    fin(V.tensor_copy(T.off2[:], T.po[:, 0:16]), "v_off2")
+    need("v", "v_off2", "s_tr")
+    fin(V.tensor_copy(T.cg[:, 0:128], T.trs[:, 0:2048].indirect(T.off2[:, 0:8])), "v_cg")
+    need("s", "v_off2", "s_tr")
+    fin(S.activation(T.cg[:, 128:256], T.trs[:, 0:2048].indirect(T.off2[:, 8:16]), F.Copy), "a_cg")
+    need("t", "v_qs", "v_cg")
+    for b in range(8):
+        if b == 4:
+            need("t", "a_cg")
+        ins = E.matmul(T.pc[:, 0:32], T.qs[:, 7 - b:135 - b], T.cg[:, 32 * b:32 * b + 32], b == 0, b == 7)
+        if b == 7:
+            fin(ins, "t_c")
+    need("v", "t_c")
+    fin(V.tensor_copy(T.sendc[:], T.pc[:, 0:32]), "v_sendc")
+    off, oe, on, ne = coarse_masks(rank)
+    mine = slice(32 * rank, 32 * rank + 32)
+    tr = [RemoteDMATransfer(dst_ids=[dst(d) for d in off], dma_engine_mask=bits(oe), remote_sem=T.sem["r_c"],
+                            srcs=[T.sendc[:]], dsts=[T.landc[:, mine] for d in off])]
+    if on:
+        tr.append(RemoteDMATransfer(dst_ids=[dst(d) for d in on], dma_engine_mask=bits(ne), remote_sem=T.sem["r_c"],
+                                    srcs=[T.sendc[:]], dsts=[T.landc[:, mine] for d in on]))
+    need("g", "v_sendc")
+    g.remote_dma_fused(tr, local_sem=T.sem["l_c"])
+    cnt["l_c"] = len(oe) + (len(ne) if on else 0)
+    got = 0
+    for r in range(n):
+        if r != rank:
+            o, e1, o2, e2 = coarse_masks(r)
+            got += len(e1) if rank in o else len(e2)
+    cnt["r_c"] = got
+
+    need("s", "v_off")
+    fin(S.activation(T.zed[:, 0:16 * A1], T.trs[:, 0:2048].indirect(T.off[:, 0:A1]), F.Copy), "a_z")
+    fin(V.tensor_scalar(T.idb[:], T.cu[:, 0:128], T.cols[:, 0:1], None, A.is_equal), "v_id")
+    fin(V.tensor_scalar(T.idf[:], T.cu[:, 0:128], T.cols[:, 0:1], None, A.is_equal), "v_id")
+    fin(V.tensor_copy(T.posf[:], T.posi[:]), "v_posf")
+    need("v", "i_m8")
+    fin(V.tensor_scalar(T.em[:], T.cm8[:], T.cols[:, 2:3], None, A.is_equal), "v_em")
+    need("v", "i_k", "i_c")
+    ms(T.coef[0:32, :], 64.0, "m_co")
+    ms(T.coef[32:64, :], 8.0, "m_co")
+    ms(T.coef[96:128, :], 8.0, "m_co")
+    fin(V.tensor_scalar(T.kmask[:], T.kcol[:], T.cols[:, 2:3], None, A.is_equal), "v_km")
+    need("v", "v_posf", "m_ft")
+    fin(V.tensor_scalar(T.feat[:, 32:64], T.feat[:, 0:32], T.posf[:, 0:1], -1.0, A.mult, A.mult), "v_feat")
+    fin(V.tensor_scalar(T.feat[:, 96:128], T.feat[:, 0:32], T.posf[:, 1:2], -1.0, A.mult, A.mult), "v_feat")
+    need("v", "v_km", "m_co")
+    fin(V.tensor_tensor(T.gee[:], T.kmask[:], T.coef[:], A.mult), "v_g")
+    need("v", "i_d")
+    ms(T.dfw[0:32, 15:16], -225.0, "m_d1")
+    need("t", "v_feat", "m_ft", "m_tr1", "i_rr", "v_neg")
+    E.matmul(T.pm[:, 128:256], T.feat[:], T.sel8[:], True, False)
+    fin(E.matmul(T.pm[:, 128:256], T.trow[:], T.rrow[:], False, True), "t_lh4")
+    need("t", "v_id", "a_cst")
+    E.matmul(T.ps[:, 0:128], T.idf[:], T.cst[:], True, False)
+    need("v", "t_lh4")
+    fin(V.tensor_copy(T.lh4[:], T.pm[:, 128:256]), "v_lh4")
+    need("v", "v_off", "s_tr")
+    fin(V.tensor_copy(T.zed[:, 16 * A2:ZL], T.trs[:, 0:2048].indirect(T.off[:, A2:ZC])), "v_z")
+
+    need("t", "v_id", "v_sendc", "r_c")
+    for i, r in enumerate([rank] + [r for r in range(n) if r != rank]):
+        src = T.sendc[:] if r == rank else T.landc[:, 32 * r:32 * r + 32]
+        ins = E.matmul(T.pe[:, 0:32], T.idb[:], src, i == 0, i == n - 1)
+        if i == n - 1:
+            fin(ins, "t_sum")
+    need("s", "t_sum")
+    fin(S.activation(T.sq[:], T.pe[:, 0:32], F.Square), "a_sq")
+    fin(S.activation(T.zed[:, 16 * A1:16 * A2], T.trs[:, 0:2048].indirect(T.off[:, A1:A2]), F.Copy), "a_z")
+    need("t", "a_sq", "v_em")
+    fin(E.matmul(T.pe[:, 64:96], T.em[:], T.sq[:], True, True), "t_e")
+    need("v", "t_e", "m_z")
+    fin(V.tensor_tensor_scan(T.cmx[:], T.pe[:, 64:96], T.zero[:], 0.0, A.max, A.max), "v_cm")
+    need("v", "v_cm")
+    fin(V.tensor_scalar(T.uu[:], T.cmx[:], T.cmx[:, 31:32], None, A.is_lt), "v_u")
+    need("v", "v_u", "m_d1")
+    fin(V.tensor_tensor(T.ud[:], T.uu[:], T.dfw[:], A.mult), "v_ud")
+    need("v", "v_ud")
+    fin(V.tensor_reduce(T.ff[:], T.ud[:], AxisListType.X, A.add), "v_f")
+    need("v", "v_f", "v_g")
+    fin(V.tensor_scalar(T.rhs[:], T.gee[:], T.ff[:, 0:1], None, A.mult), "v_rhs")
+    need("t", "v_rhs", "v_lh4")
+    fin(E.matmul(T.ps[:, 0:128], T.lh4[:], T.rhs[:], False, True), "t_s")
+    need("t", "m_lw1")
+    for h in range(2):
+        k0 = korder[half * h]
+        fin(E.matmul(T.pm[0:1, 300 + k0:304 + k0], T.lhw[:], T.rhs[:, 64 * h:64 * h + 8:2], True, True), "t_w")
+    need("v", "t_s")
+    for h in range(2):
+        c = slice(64 * h, 64 * h + 64)
+        fin(V.tensor_scalar(T.lst[:, c], T.ps[:, c], 0.0625, -15.0 / 32, A.mult, A.add), "v_l%d" % h)
+
+    need("v", "v_z", "a_z")
+    need("s", "v_z", "a_z")
+    for h in range(2):
+        o = 1024 * h
+        need("s", "v_l%d" % h)
+        fin(S.activation(T.fg[:, o:o + 512], T.zed[:, 0:ZL].indirect(T.lst[:, 64 * h:64 * h + 32]), F.Copy), "a_g%d" % h)
+        need("v", "v_l%d" % h)
+        fin(V.tensor_copy(T.fg[:, o + 512:o + 1024], T.zed[:, 0:ZL].indirect(T.lst[:, 64 * h + 32:64 * h + 64])), "v_g%d" % h)
+    for h in range(2):
+        acc = T["pf%d" % h]
+        o = 1024 * h
+        need("t", "a_g%d" % h)
+        for j in range(8):
+            if j == 4:
+                need("t", "v_g%d" % h)
+            ins = E.matmul(acc[:, 0:128], T.qs[:, 7 - j:135 - j], T.fg[:, o + 128 * j:o + 128 * j + 128], j == 0, j == 7)
+            if j == 7:
+                fin(ins, "t_f%d" % h)
+        need("v", "t_f%d" % h)
+        fin(V.tensor_copy(T.sendf[:, 128 * h:128 * h + 128], acc[:, 0:128]), "v_e%d" % h)
+
+    for h in range(2):
+        dests = halves(rank)[h]
+        em = masks(rank, dests)
+        need("g", "v_e%d" % h)
+        tr = []
+        for d in dests:
+            k = korder.index(d)
+            tr.append(RemoteDMATransfer(dst_ids=[dst(d)], dma_engine_mask=bits(em[d]), remote_sem=T.sem["r_f%d" % h],
+                                        srcs=[T.sendf[:, 32 * k:32 * k + 32]], dsts=[T.landf[:, mine]]))
+            cnt["l_f"] = cnt.get("l_f", 0) + len(em[d])
+        g.remote_dma_fused(tr, local_sem=T.sem["l_f"])
+    groups = []
+    for h in range(2):
+        rs = [r for r in range(n) if r != rank and rank in halves(r)[h]]
+        cnt["r_f%d" % h] = sum(len(masks(r, halves(r)[h])[rank]) for r in rs)
+        groups.append(rs)
+
+    need("v", "t_w", "i_kw")
+    fin(V.tensor_tensor(T.wout[:], T.pm[0:1, 300:308], T.kw[:], A.add), "v_w")
+    need("y", "v_w")
+    fin(Y.dma_start(T.w[:], T.wout[:]), "s_w", 16)
+
+    need("t", "v_e1")
+    k = korder.index(rank)
+    E.matmul(T.pc[:, 0:32], T.idb[:], T.sendf[:, 32 * k:32 * k + 32], True, False)
+    for h in range(2):
+        need("t", "r_f%d" % h)
+        for i, r in enumerate(groups[h]):
+            last = h == 1 and i == len(groups[h]) - 1
+            ins = E.matmul(T.pc[:, 0:32], T.idb[:], T.landf[:, 32 * r:32 * r + 32], False, last)
+            if last:
+                fin(ins, "t_y")
+    need("v", "t_y")
+    fin(V.tensor_copy(T.yout[:], T.pc[:, 0:32]), "v_y")
+    need("y", "v_y")
+    fin(Y.dma_start(T.y[:], T.yout[:]), "s_y", 16)
+    need("y", "s_w", "s_y")
+    done = {}
+    for (q, nm), k in seen.items():
+        done[nm] = max(done.get(nm, 0), k)
+    for nm in list(cnt):
+        if done.get(nm, 0) < cnt[nm]:
+            need("g", nm)

@@ -3,40 +3,41 @@ from concourse.mybir import AluOpType, AxisListType, ActivationFunctionType
 
 ZC = 510
 ZL = 16 * ZC
-A1, A2 = 240, 288
+A1, A2 = 236, 292
 
 F32, B16, H16, I32, U16 = "float32", "bfloat16", "float16", "int32", "uint16"
 SCRATCH = {
     "pin": ("sbuf", [128, 8, 64], I32), "pf": ("sbuf", [128, 4, 8, 16], H16),
     "posi": ("sbuf", [8, 2], I32), "posb": ("sbuf", [8, 2], B16), "posf": ("sbuf", [8, 2], F32),
     "feat": ("sbuf", [8, 128], B16), "gsel": ("sbuf", [8, 128], F32), "sel8": ("sbuf", [8, 128], B16),
-    "rrow": ("sbuf", [1, 128], B16), "trow": ("sbuf", [1, 128], B16),
+    "rrow": ("sbuf", [1, 128], B16), "trow": ("sbuf", [1, 128], B16), "cgt": ("sbuf", [16, 128], F32),
     "kw": ("sbuf", [1, 8], F32), "wout": ("sbuf", [1, 8], F32),
 }
 for _nm, _w, _t in [
         ("trs", 2048, B16), ("nat", 512, F32), ("off", 512, U16), ("zed", ZL, B16), ("ints", 4, I32), ("cols", 4, F32),
-        ("colg", 1, F32), ("col8", 1, F32), ("cu", 144, F32), ("cm8", 128, F32), ("aj", 256, F32), ("bj", 256, F32),
-        ("qg", 144, H16), ("qs", 144, B16), ("idb", 128, B16), ("idh", 128, H16), ("idf", 128, F32), ("em", 128, F32),
-        ("zero", 32, F32), ("dfw", 32, F32), ("kcol", 128, F32), ("kmask", 128, F32), ("coef", 128, F32),
+        ("col8", 1, F32), ("cu", 144, F32), ("cm8", 128, F32), ("aj", 256, F32), ("bj", 256, F32),
+        ("bsel", 8, H16), ("qs", 144, B16), ("idh", 128, H16), ("idf", 128, F32), ("em", 128, F32),
+        ("zero", 32, F32), ("dfw", 32, F32), ("kcol", 128, F32), ("ccol", 1, F32), ("coef", 128, F32),
         ("gee", 128, B16), ("kyi", 128, F32), ("kysq", 128, F32), ("cst", 128, F32), ("lh4", 128, B16), ("lhw", 1, B16),
-        ("neg", 2, F32), ("b8", 2, F32), ("b8s", 2, F32), ("xx", 256, F32), ("yy", 256, F32), ("ss", 256, I32),
+        ("neg", 2, F32), ("b8", 2, F32), ("b8s", 2, F32), ("yy", 256, F32), ("ss", 256, I32),
         ("rj", 256, I32), ("mask", 256, F32), ("dxc", 1, F32), ("rx2", 1, F32), ("dyc", 16, F32), ("cidx", 16, U16),
-        ("yg", 256, H16), ("off2", 16, U16), ("cg", 256, B16), ("sendc", 32, B16), ("landc", 256, B16), ("sq", 32, F32),
+        ("yg", 256, H16), ("off2", 16, U16), ("cg", 256, B16), ("sendc", 32, H16), ("landc", 256, H16), ("sq", 32, F32),
         ("cmx", 32, F32), ("uu", 32, F32), ("ud", 32, F32), ("ff", 1, F32), ("rhs", 128, B16), ("lst", 128, U16),
-        ("fg", 2048, B16), ("sendf", 256, B16), ("landf", 256, B16), ("yout", 32, F32)]:
+        ("fg", 2048, B16), ("sendf", 256, H16), ("landf", 256, H16), ("yout", 32, F32)]:
     SCRATCH[_nm] = ("sbuf", [128, _w], _t)
 for _nm in ["pt", "po", "pc", "pe", "ps", "pf0", "pf1", "pm"]:
     SCRATCH[_nm] = ("psum", [128, 512], F32)
 SEMAPHORES = ["s_pos", "s_tau", "s_tr", "s_w", "s_y",
               "i_p", "i_sel", "i_aj", "i_bj", "i_u", "i_m8", "i_d", "i_k", "i_c", "i_ky", "i_rr", "i_kw",
-              "m_z", "m_d0", "m_d1", "m_co", "m_lw0", "m_lw1", "m_ft", "m_tr0", "m_tr1",
-              "v_int", "v_col", "v_c2", "v_sel", "v_qg", "v_qs", "v_id", "v_idh", "v_em", "v_km", "v_g", "v_posb",
-              "v_posf", "v_neg", "v_feat", "v_cidx", "v_ss", "v_rj", "v_mask", "v_pf", "v_yg", "v_off", "v_off2", "v_cg",
-              "v_sendc", "v_lh4", "v_z", "v_cm", "v_u", "v_ud", "v_f", "v_rhs", "v_l0", "v_l1", "v_g0", "v_g1", "v_e0",
-              "v_e1", "v_w", "v_y",
-              "a_xx", "a_dc", "a_rx", "a_ky", "a_cst", "a_n", "a_cg", "a_z", "a_sq", "a_g0", "a_g1",
-              "t_pos", "t_t", "t_off", "t_c", "t_lh4", "t_sum", "t_e", "t_s", "t_w", "t_f0", "t_f1", "t_y",
-              "r_c", "r_f0", "r_f1", "l_c", "l_f"]
+              "m_z", "m_d0", "m_d1", "m_co", "m_c2", "m_lw0", "m_lw1", "m_ft", "m_tr0", "m_tr1",
+              "v_int", "v_col", "v_c2", "v_sel", "v_bs", "v_qs", "v_id", "v_idh", "v_em", "v_km", "v_g", "v_posb",
+              "v_posf", "v_feat", "v_cidx", "v_ss", "v_rj", "v_mask", "v_pf0", "v_pf1", "v_pf2", "v_pf3", "v_yg",
+              "v_off", "v_off2", "v_cg", "v_sendc", "v_z", "v_cm", "v_u", "v_ud", "v_f", "v_rhs", "v_l0", "v_l1",
+              "v_g0", "v_g1", "v_g2", "v_g3", "v_e0", "v_e1", "v_w", "v_y",
+              "a_neg", "a_xx", "a_dc", "a_rx", "a_ky", "a_cst", "a_n", "a_lh4", "a_cgt", "a_cg", "a_z", "a_sq",
+              "a_g0", "a_g1", "a_g2", "a_g3",
+              "t_pos", "t_t0", "t_t1", "t_t2", "t_t3", "t_o1", "t_off", "t_c", "t_lh4", "t_sum", "t_e", "t_s", "t_w",
+              "t_f0", "t_f1", "t_y", "l_c", "l_f"] + ["r_c%d" % _i for _i in range(8)] + ["r_f%d" % _i for _i in range(8)]
 
 
 def rank_program(g, core, T, topo):
@@ -68,6 +69,10 @@ def rank_program(g, core, T, topo):
     def bits(es):
         return sum(1 << e for e in es)
 
+    def far(r, d):
+        a, b = topo.chip(cores[r]), topo.chip(cores[d])
+        return (3 if a == b else 2 if topo.same_plane(a, b) else 1 if topo.mates(a, b) else 0, r ^ d)
+
     def masks(r, dests):
         src = cores[r]
         off = [d for d in dests if topo.chip(cores[d]) != topo.chip(src)]
@@ -86,10 +91,13 @@ def rank_program(g, core, T, topo):
         o = order(r)
         return [d for d in o[:half] if d != r], [d for d in o[half:] if d != r]
 
+    def others(r):
+        return sorted([d for d in range(n) if d != r], key=lambda d: far(r, d))
+
     def coarse_masks(r):
         src = cores[r]
-        off = [d for d in range(n) if topo.chip(cores[d]) != topo.chip(src)]
-        on = [d for d in range(n) if d != r and d not in off]
+        off = [d for d in others(r) if topo.chip(cores[d]) != topo.chip(src)]
+        on = [d for d in others(r) if d not in off]
         oe = topo.engines(src, cores[off[0]])
         ne = [e for e in topo.engines(src, cores[on[0]]) if e not in oe][:2] if on else []
         return off, oe, on, ne
@@ -102,10 +110,9 @@ def rank_program(g, core, T, topo):
 
     fin(Y.dma_start(T.posi[:], T.pos[:]), "s_pos", 16)
     for s in range(8):
-        q = Y if s < 4 else S
+        q = Y if s < 3 else S
         fin(q.dma_start(T.pin[:, s, :], T.tau[s:s + 1, :]), "s_tau", 16)
-    fin(Y.dma_start(T.trs[0:64, :], T.tr[0:64, :]), "s_tr", 16)
-    fin(S.dma_start(T.trs[64:128, :], T.tr[64:128, :]), "s_tr", 16)
+    fin(S.dma_start(T.trs[:], T.tr[:]), "s_tr", 16)
 
     def iota(ap, pat, base, cm, name):
         fin(g.iota(ap, pat, base, cm, allow_small_or_imprecise_dtypes=True), name)
@@ -115,92 +122,112 @@ def rank_program(g, core, T, topo):
     iota(T.aj[:], [[0, 16], [1, 16]], 0, 0, "i_aj")
     iota(T.bj[:], [[1, 16], [0, 16]], 0, 0, "i_bj")
     iota(T.cu[:], [[1, 144]], 0, 0, "i_u")
-    iota(T.cm8[:], [[0, 16], [1, 8]], 0, 0, "i_m8")
-    for h in range(2):
-        k0 = korder[half * h]
-        c = slice(64 * h, 64 * h + 64)
-        iota(T.kcol[:, c], [[0, 8], [1, 4], [0, 2]], k0, 0, "i_k")
-        iota(T.coef[:, c], [[16, 8], [256, 4], [8, 2]], 64 + 256 * k0, 0, "i_c")
-        iota(T.kyi[:, c], [[2, 8], [32, 4], [1, 2]], 32 * k0, 0, "i_ky")
-    iota(T.dfw[0:32, :], [[0, 2], [2, 16]], 1, 0, "i_d")
     iota(T.rrow[:], [[0, 8], [1, 16]], 0, 0, "i_rr")
+    iota(T.cm8[:], [[0, 16], [1, 8]], 0, 0, "i_m8")
+    hs = [(korder[half * h], slice(64 * h, 64 * h + 64)) for h in range(2)]
+    for k0, c in hs:
+        iota(T.kyi[:, c], [[2, 8], [32, 4], [1, 2]], 32 * k0, 0, "i_ky")
+    for k0, c in hs:
+        iota(T.kcol[:, c], [[0, 8], [1, 4], [0, 2]], k0, 0, "i_k")
+    for k0, c in hs:
+        iota(T.coef[:, c], [[2, 8], [32, 4], [1, 2]], 8 + 32 * k0, 0, "i_c")
+    iota(T.dfw[0:32, :], [[0, 2], [2, 16]], 1, 0, "i_d")
     iota(T.kw[:], [[32, 8]], 0, 0, "i_kw")
 
     def ms(ap, x, name):
         fin(V.memset(ap, x), name)
 
-    ms(T.zero[:], 0.0, "m_z")
+    ms(T.feat[:], 1.0, "m_ft")
+    ms(T.trow[:], 0.0, "m_tr0")
+    ms(T.ccol[:], 8.0, "m_co")
     ms(T.dfw[32:64, :], 1.0, "m_d0")
     ms(T.dfw[64:128, :], 0.0, "m_d0")
     ms(T.lhw[:], 0.0, "m_lw0")
-    ms(T.feat[:], 1.0, "m_ft")
-    ms(T.trow[:], 0.0, "m_tr0")
-    need("v", "m_d0", "m_lw0", "m_tr0")
-    ms(T.dfw[32:64, 15:16], -15.0, "m_d1")
-    ms(T.dfw[64:128, 15:16], 1.0, "m_d1")
-    ms(T.lhw[32:64, :], 1.0 / 32, "m_lw1")
-    ms(T.lhw[96:128, :], 0.5, "m_lw1")
-    ms(T.trow[:, 32:64], 1.0, "m_tr1")
+    ms(T.zero[:], 0.0, "m_z")
     need("v", "i_p")
     fin(V.tensor_scalar(T.ints[:, 1:2], T.ints[:, 0:1], 15, None, A.bitwise_and), "v_int")
     fin(V.tensor_scalar(T.ints[:, 2:3], T.ints[:, 0:1], 7, None, A.bitwise_and), "v_int")
     fin(V.tensor_scalar(T.ints[:, 3:4], T.ints[:, 0:1], 112, None, A.bitwise_and), "v_int")
+    need("v", "m_d0", "m_lw0", "m_tr0", "m_co")
+    ms(T.trow[:, 32:64], 1.0, "m_tr1")
+    ms(T.ccol[0:32, :], 64.0, "m_c2")
     need("v", "v_int")
     fin(V.tensor_copy(T.cols[:], T.ints[:]), "v_col")
-    need("v", "v_col")
-    fin(V.tensor_scalar(T.colg[:], T.cols[:, 3:4], 15.0, None, A.add), "v_c2")
-    fin(V.tensor_scalar(T.col8[:], T.cols[:, 1:2], 8.0, 7.0, A.mult, A.add), "v_c2")
     need("v", "i_sel")
     fin(V.tensor_scalar(T.sel8[:], T.gsel[:], 0.0, None, A.is_equal), "v_sel")
+    need("v", "v_col")
+    fin(V.tensor_scalar(T.col8[:], T.cols[:, 1:2], 8.0, 7.0, A.mult, A.add), "v_c2")
+    ms(T.dfw[32:64, 15:16], -15.0, "m_d1")
+    ms(T.dfw[64:128, 15:16], 1.0, "m_d1")
+    ms(T.lhw[32:64, :], 1.0 / 32, "m_lw1")
+    ms(T.lhw[96:128, :], 0.5, "m_lw1")
     need("v", "s_pos")
     fin(V.tensor_copy(T.posb[:], T.posi[:]), "v_posb")
+    fin(V.tensor_copy(T.posf[:], T.posi[:]), "v_posf")
     need("t", "v_sel", "v_posb")
     fin(E.matmul(T.pm[:, 0:2], T.sel8[:], T.posb[:], True, True), "t_pos")
     need("v", "v_c2", "i_u")
     fin(V.tensor_scalar(T.idh[:], T.cu[:, 0:128], T.cols[:, 0:1], None, A.is_equal), "v_idh")
-    need("v", "t_pos")
-    fin(V.tensor_scalar(T.b8[:], T.pm[:, 0:2], -1.0, 8.0, A.mult, A.add), "v_neg")
-    fin(V.tensor_scalar(T.b8s[:], T.pm[:, 0:2], -0.0625, 0.5, A.mult, A.add), "v_neg")
-    fin(V.tensor_scalar(T.neg[:], T.pm[:, 0:2], -1.0, None, A.mult), "v_neg")
-    need("s", "v_neg", "i_aj", "i_bj", "v_col", "i_u")
+    need("v", "v_posf", "m_ft")
+    fin(V.tensor_scalar(T.feat[:, 32:64], T.feat[:, 0:32], T.posf[:, 0:1], -1.0, A.mult, A.mult), "v_feat")
+    fin(V.tensor_scalar(T.feat[:, 96:128], T.feat[:, 0:32], T.posf[:, 1:2], -1.0, A.mult, A.mult), "v_feat")
+    fin(V.tensor_scalar(T.idf[:], T.cu[:, 0:128], T.cols[:, 0:1], None, A.is_equal), "v_id")
+    need("s", "t_pos")
+    fin(S.activation(T.b8[:], T.pm[:, 0:2], F.Copy, bias=8.0, scale=-1.0), "a_neg")
+    fin(S.activation(T.b8s[:], T.pm[:, 0:2], F.Copy, bias=0.5, scale=-0.0625), "a_neg")
+    fin(S.activation(T.neg[:], T.pm[:, 0:2], F.Copy, scale=-1.0), "a_neg")
+    need("s", "a_neg", "i_aj", "i_bj", "v_col", "i_u")
+    fin(S.activation(T.pf1[:, 0:256], T.aj[:], F.Square, bias=T.b8[:, 0:1], scale=16.0), "a_xx")
+    fin(S.activation(T.yy[:], T.bj[:], F.Square, bias=T.b8[:, 1:2], scale=16.0), "a_xx")
     fin(S.activation(T.dyc[:], T.cu[:, 0:16], F.Square, bias=T.b8s[:, 1:2]), "a_dc")
     fin(S.activation(T.dxc[:], T.cols[:, 1:2], F.Square, bias=T.b8s[:, 0:1]), "a_dc")
-    fin(S.activation(T.xx[:], T.aj[:], F.Square, bias=T.b8[:, 0:1], scale=16.0), "a_xx")
-    fin(S.activation(T.yy[:], T.bj[:], F.Square, bias=T.b8[:, 1:2], scale=16.0), "a_xx")
     fin(S.activation(T.rx2[:], T.cols[:, 1:2], F.Square, bias=T.neg[:, 0:1]), "a_rx")
-    need("s", "i_ky")
-    fin(S.activation(T.kysq[:], T.kyi[:], F.Square, bias=T.neg[:, 1:2]), "a_ky")
-    need("s", "a_rx", "a_ky")
-    fin(S.activation(T.cst[:], T.kysq[:], F.Identity, bias=T.rx2[:, 0:1]), "a_cst")
-    fin(V.tensor_scalar(T.qg[:], T.cu[:], T.colg[:, 0:1], None, A.is_equal), "v_qg")
-    need("v", "a_dc")
-    fin(V.tensor_scalar(T.cidx[:], T.dyc[:], T.dxc[:, 0:1], -255.0 / 512, A.add, A.add), "v_cidx")
     need("v", "a_xx")
-    fin(V.tensor_tensor(T.ss[:], T.xx[:], T.yy[:], A.add), "v_ss")
-    need("v", "v_ss")
-    fin(V.tensor_scalar(T.rj[:], T.ss[:], 4, 15, A.arith_shift_right, A.bitwise_and), "v_rj")
-    need("v", "v_rj")
-    fin(V.tensor_scalar(T.mask[:], T.rj[:], T.cols[:, 1:2], None, A.is_equal), "v_mask")
+    fin(V.tensor_tensor(T.ss[:], T.pf1[:, 0:256], T.yy[:], A.add), "v_ss")
+
+    def piece(cb):
+        fin(V.tensor_copy(T.pf[:, cb, :, :], T.pin[:, :, 16 * cb:16 * cb + 16]), "v_pf%d" % cb)
+        bank = T[["pt", "po", "pc", "pe"][cb]]
+        need("t", "v_pf%d" % cb, "v_idh")
+        fin(E.matmul(bank[:, 0:128], T.pf[:, cb, :, :], T.idh[:], True, True), "t_t%d" % cb)
+        need("s", "t_t%d" % cb)
+        fin(S.activation(T.nat[:, cb::4], bank[:, 0:128], F.Copy), "a_n")
 
     need("v", "s_tau")
-    for cb in range(4):
-        fin(V.tensor_copy(T.pf[:, cb, :, :], T.pin[:, :, 16 * cb:16 * cb + 16]), "v_pf")
-    need("t", "v_pf", "v_idh")
-    for cb in range(4):
-        fin(E.matmul(T.pt[:, cb::4], T.pf[:, cb, :, :], T.idh[:], True, True), "t_t")
-    need("s", "t_t")
-    fin(S.activation(T.nat[:], T.pt[:], F.Copy), "a_n")
+    piece(0)
+    piece(1)
+    need("v", "v_ss")
+    fin(V.tensor_scalar(T.rj[:], T.ss[:], 4, 15, A.arith_shift_right, A.bitwise_and), "v_rj")
+    piece(2)
+    piece(3)
+    need("v", "v_rj")
+    fin(V.tensor_scalar(T.mask[:], T.rj[:], T.cols[:, 1:2], None, A.is_equal), "v_mask")
+    need("v", "a_dc")
+    fin(V.tensor_scalar(T.cidx[:], T.dyc[:], T.dxc[:, 0:1], -255.0 / 512, A.add, A.add), "v_cidx")
+    fin(V.tensor_scalar(T.bsel[:], T.cu[:, 0:128:16], T.cols[:, 3:4], None, A.is_equal), "v_bs")
     fin(V.tensor_scalar(T.qs[:], T.cu[:], T.col8[:, 0:1], None, A.is_equal), "v_qs")
+    need("t", "v_feat", "m_ft", "m_tr1", "i_rr", "a_neg")
+    E.matmul(T.pm[:, 128:256], T.feat[:], T.sel8[:], True, False)
+    fin(E.matmul(T.pm[:, 128:256], T.trow[:], T.rrow[:], False, True), "t_lh4")
+    need("s", "t_lh4")
+    fin(S.activation(T.lh4[:], T.pm[:, 128:256], F.Copy), "a_lh4")
     need("v", "a_n", "v_cidx", "v_mask")
     fin(V.tensor_tensor(T.yg[:], T.nat[:, 0:512].indirect(T.cidx[:, 0:16]), T.mask[:], A.mult), "v_yg")
-    need("t", "v_yg", "v_qg")
+    need("t", "v_yg", "v_bs", "a_n")
     for r in range(16):
-        ins = E.matmul(T.po[:, 0:16], T.qg[:, 15 - r:143 - r], T.yg[:, r::16], r == 0, r == 15)
-        if r == 15:
-            fin(ins, "t_off")
+        ins = E.matmul(T.po[0:16, r:128:16], T.yg[:, r::16], T.bsel[:], True, True)
+    fin(ins, "t_o1")
+    need("s", "t_o1")
+    fin(S.activation(T.cgt[:], T.po[0:16, 0:128], F.Copy), "a_cgt")
+    need("t", "a_cgt", "v_id")
+    fin(E.matmul(T.pt[:, 0:16], T.cgt[:], T.idf[0:16, 0:16], True, True), "t_off")
+    need("s", "i_ky", "a_rx")
+    fin(S.activation(T.kysq[:], T.kyi[:], F.Square, bias=T.neg[:, 1:2]), "a_ky")
+    need("s", "a_ky")
+    fin(S.activation(T.cst[:], T.kysq[:], F.Identity, bias=T.rx2[:, 0:1]), "a_cst")
     fin(V.tensor_copy(T.off[:], T.nat[:]), "v_off")
     need("v", "t_off")
-    fin(V.tensor_copy(T.off2[:], T.po[:, 0:16]), "v_off2")
+    fin(V.tensor_copy(T.off2[:], T.pt[:, 0:16]), "v_off2")
     need("v", "v_off2", "s_tr")
     fin(V.tensor_copy(T.cg[:, 0:128], T.trs[:, 0:2048].indirect(T.off2[:, 0:8])), "v_cg")
     need("s", "v_off2", "s_tr")
@@ -212,64 +239,48 @@ def rank_program(g, core, T, topo):
         ins = E.matmul(T.pc[:, 0:32], T.qs[:, 7 - b:135 - b], T.cg[:, 32 * b:32 * b + 32], b == 0, b == 7)
         if b == 7:
             fin(ins, "t_c")
+    need("v", "i_m8")
+    fin(V.tensor_scalar(T.em[:], T.cm8[:], T.cols[:, 2:3], None, A.is_equal), "v_em")
+    need("v", "i_k", "m_c2")
+    fin(V.tensor_scalar(T.gee[:], T.kcol[:], T.cols[:, 2:3], T.ccol[:, 0:1], A.is_equal, A.mult), "v_km")
     need("v", "t_c")
     fin(V.tensor_copy(T.sendc[:], T.pc[:, 0:32]), "v_sendc")
     off, oe, on, ne = coarse_masks(rank)
     mine = slice(32 * rank, 32 * rank + 32)
-    tr = [RemoteDMATransfer(dst_ids=[dst(d) for d in off], dma_engine_mask=bits(oe), remote_sem=T.sem["r_c"],
+    rc = T.sem["r_c%d" % rank]
+    tr = [RemoteDMATransfer(dst_ids=[dst(d) for d in off], dma_engine_mask=bits(oe), remote_sem=rc,
                             srcs=[T.sendc[:]], dsts=[T.landc[:, mine] for d in off])]
     if on:
-        tr.append(RemoteDMATransfer(dst_ids=[dst(d) for d in on], dma_engine_mask=bits(ne), remote_sem=T.sem["r_c"],
+        tr.append(RemoteDMATransfer(dst_ids=[dst(d) for d in on], dma_engine_mask=bits(ne), remote_sem=rc,
                                     srcs=[T.sendc[:]], dsts=[T.landc[:, mine] for d in on]))
     need("g", "v_sendc")
     g.remote_dma_fused(tr, local_sem=T.sem["l_c"])
     cnt["l_c"] = len(oe) + (len(ne) if on else 0)
-    got = 0
-    for r in range(n):
-        if r != rank:
-            o, e1, o2, e2 = coarse_masks(r)
-            got += len(e1) if rank in o else len(e2)
-    cnt["r_c"] = got
+    for r in others(rank):
+        o, e1, o2, e2 = coarse_masks(r)
+        cnt["r_c%d" % r] = len(e1) if rank in o else len(e2)
 
     need("s", "v_off")
     fin(S.activation(T.zed[:, 0:16 * A1], T.trs[:, 0:2048].indirect(T.off[:, 0:A1]), F.Copy), "a_z")
-    fin(V.tensor_scalar(T.idb[:], T.cu[:, 0:128], T.cols[:, 0:1], None, A.is_equal), "v_id")
-    fin(V.tensor_scalar(T.idf[:], T.cu[:, 0:128], T.cols[:, 0:1], None, A.is_equal), "v_id")
-    fin(V.tensor_copy(T.posf[:], T.posi[:]), "v_posf")
-    need("v", "i_m8")
-    fin(V.tensor_scalar(T.em[:], T.cm8[:], T.cols[:, 2:3], None, A.is_equal), "v_em")
-    need("v", "i_k", "i_c")
-    ms(T.coef[0:32, :], 64.0, "m_co")
-    ms(T.coef[32:64, :], 8.0, "m_co")
-    ms(T.coef[96:128, :], 8.0, "m_co")
-    fin(V.tensor_scalar(T.kmask[:], T.kcol[:], T.cols[:, 2:3], None, A.is_equal), "v_km")
-    need("v", "v_posf", "m_ft")
-    fin(V.tensor_scalar(T.feat[:, 32:64], T.feat[:, 0:32], T.posf[:, 0:1], -1.0, A.mult, A.mult), "v_feat")
-    fin(V.tensor_scalar(T.feat[:, 96:128], T.feat[:, 0:32], T.posf[:, 1:2], -1.0, A.mult, A.mult), "v_feat")
-    need("v", "v_km", "m_co")
-    fin(V.tensor_tensor(T.gee[:], T.kmask[:], T.coef[:], A.mult), "v_g")
-    need("v", "i_d")
-    ms(T.dfw[0:32, 15:16], -225.0, "m_d1")
-    need("t", "v_feat", "m_ft", "m_tr1", "i_rr", "v_neg")
-    E.matmul(T.pm[:, 128:256], T.feat[:], T.sel8[:], True, False)
-    fin(E.matmul(T.pm[:, 128:256], T.trow[:], T.rrow[:], False, True), "t_lh4")
     need("t", "v_id", "a_cst")
     E.matmul(T.ps[:, 0:128], T.idf[:], T.cst[:], True, False)
-    need("v", "t_lh4")
-    fin(V.tensor_copy(T.lh4[:], T.pm[:, 128:256]), "v_lh4")
+    need("v", "v_km", "i_c", "i_d")
+    fin(V.tensor_tensor(T.gee[64:96, :], T.gee[64:96, :], T.coef[64:96, :], A.mult), "v_g")
+    ms(T.dfw[0:32, 15:16], -225.0, "m_d1")
     need("v", "v_off", "s_tr")
     fin(V.tensor_copy(T.zed[:, 16 * A2:ZL], T.trs[:, 0:2048].indirect(T.off[:, A2:ZC])), "v_z")
 
-    need("t", "v_id", "v_sendc", "r_c")
-    for i, r in enumerate([rank] + [r for r in range(n) if r != rank]):
-        src = T.sendc[:] if r == rank else T.landc[:, 32 * r:32 * r + 32]
-        ins = E.matmul(T.pe[:, 0:32], T.idb[:], src, i == 0, i == n - 1)
-        if i == n - 1:
+    need("t", "v_sendc")
+    E.matmul(T.pe[:, 0:32], T.idh[:], T.sendc[:], True, False)
+    for i, r in enumerate([r for r in others(rank) if r in on] + [r for r in others(rank) if r not in on]):
+        need("t", "r_c%d" % r)
+        ins = E.matmul(T.pe[:, 0:32], T.idh[:], T.landc[:, 32 * r:32 * r + 32], False, i == n - 2)
+        if i == n - 2:
             fin(ins, "t_sum")
     need("s", "t_sum")
     fin(S.activation(T.sq[:], T.pe[:, 0:32], F.Square), "a_sq")
-    fin(S.activation(T.zed[:, 16 * A1:16 * A2], T.trs[:, 0:2048].indirect(T.off[:, A1:A2]), F.Copy), "a_z")
     need("t", "a_sq", "v_em")
+    fin(S.activation(T.zed[:, 16 * A1:16 * A2], T.trs[:, 0:2048].indirect(T.off[:, A1:A2]), F.Copy), "a_z")
     fin(E.matmul(T.pe[:, 64:96], T.em[:], T.sq[:], True, True), "t_e")
     need("v", "t_e", "m_z")
     fin(V.tensor_tensor_scan(T.cmx[:], T.pe[:, 64:96], T.zero[:], 0.0, A.max, A.max), "v_cm")
@@ -281,54 +292,70 @@ def rank_program(g, core, T, topo):
     fin(V.tensor_reduce(T.ff[:], T.ud[:], AxisListType.X, A.add), "v_f")
     need("v", "v_f", "v_g")
     fin(V.tensor_scalar(T.rhs[:], T.gee[:], T.ff[:, 0:1], None, A.mult), "v_rhs")
-    need("t", "v_rhs", "v_lh4")
+    need("t", "v_rhs", "a_lh4")
     fin(E.matmul(T.ps[:, 0:128], T.lh4[:], T.rhs[:], False, True), "t_s")
     need("t", "m_lw1")
-    for h in range(2):
-        k0 = korder[half * h]
-        fin(E.matmul(T.pm[0:1, 300 + k0:304 + k0], T.lhw[:], T.rhs[:, 64 * h:64 * h + 8:2], True, True), "t_w")
+    for k0, c in hs:
+        fin(E.matmul(T.pm[0:1, 300 + k0:304 + k0], T.lhw[:], T.rhs[:, c.start:c.start + 8:2], True, True), "t_w")
     need("v", "t_s")
-    for h in range(2):
-        c = slice(64 * h, 64 * h + 64)
+    for h, (k0, c) in enumerate(hs):
         fin(V.tensor_scalar(T.lst[:, c], T.ps[:, c], 0.0625, -15.0 / 32, A.mult, A.add), "v_l%d" % h)
 
     need("v", "v_z", "a_z")
     need("s", "v_z", "a_z")
-    for h in range(2):
-        o = 1024 * h
-        need("s", "v_l%d" % h)
-        fin(S.activation(T.fg[:, o:o + 512], T.zed[:, 0:ZL].indirect(T.lst[:, 64 * h:64 * h + 32]), F.Copy), "a_g%d" % h)
-        need("v", "v_l%d" % h)
-        fin(V.tensor_copy(T.fg[:, o + 512:o + 1024], T.zed[:, 0:ZL].indirect(T.lst[:, 64 * h + 32:64 * h + 64])), "v_g%d" % h)
-    for h in range(2):
+
+    def pick(q, h, j):
+        lo = 64 * h + 8 * j
+        o = T.fg[:, 16 * lo:16 * lo + 256]
+        w = T.zed[:, 0:ZL].indirect(T.lst[:, lo:lo + 16])
+        need(q, "v_l%d" % h)
+        if q == "s":
+            fin(S.activation(o, w, F.Copy), "a_g%d" % (2 * h + j // 2))
+        else:
+            fin(V.tensor_copy(o, w), "v_g%d" % (2 * h + j // 2 - 2))
+
+    def add_up(h):
         acc = T["pf%d" % h]
-        o = 1024 * h
-        need("t", "a_g%d" % h)
-        for j in range(8):
-            if j == 4:
-                need("t", "v_g%d" % h)
-            ins = E.matmul(acc[:, 0:128], T.qs[:, 7 - j:135 - j], T.fg[:, o + 128 * j:o + 128 * j + 128], j == 0, j == 7)
-            if j == 7:
-                fin(ins, "t_f%d" % h)
+        for i, j in enumerate([0, 4, 2, 6]):
+            need("t", ("a_g%d" % (2 * h + j // 2)) if j < 4 else ("v_g%d" % (2 * h + j // 2 - 2)))
+            for jj in (j, j + 1):
+                o = 1024 * h + 128 * jj
+                ins = E.matmul(acc[:, 0:128], T.qs[:, 7 - jj:135 - jj], T.fg[:, o:o + 128], i == 0 and jj == j, i == 3 and jj > j)
+        fin(ins, "t_f%d" % h)
+
+    def ready(h):
         need("v", "t_f%d" % h)
-        fin(V.tensor_copy(T.sendf[:, 128 * h:128 * h + 128], acc[:, 0:128]), "v_e%d" % h)
+        fin(V.tensor_copy(T.sendf[:, 128 * h:128 * h + 128], T["pf%d" % h][:, 0:128]), "v_e%d" % h)
 
     for h in range(2):
-        dests = halves(rank)[h]
+        pick("s", h, 0)
+        pick("s", h, 2)
+    pick("v", 0, 4)
+    pick("v", 0, 6)
+    add_up(0)
+    pick("v", 1, 4)
+    ready(0)
+    pick("v", 1, 6)
+    add_up(1)
+    ready(1)
+
+    for h in range(2):
+        dests = sorted(halves(rank)[h], key=lambda d: far(rank, d))
         em = masks(rank, dests)
         need("g", "v_e%d" % h)
         tr = []
         for d in dests:
             k = korder.index(d)
-            tr.append(RemoteDMATransfer(dst_ids=[dst(d)], dma_engine_mask=bits(em[d]), remote_sem=T.sem["r_f%d" % h],
+            tr.append(RemoteDMATransfer(dst_ids=[dst(d)], dma_engine_mask=bits(em[d]), remote_sem=T.sem["r_f%d" % rank],
                                         srcs=[T.sendf[:, 32 * k:32 * k + 32]], dsts=[T.landf[:, mine]]))
             cnt["l_f"] = cnt.get("l_f", 0) + len(em[d])
         g.remote_dma_fused(tr, local_sem=T.sem["l_f"])
-    groups = []
-    for h in range(2):
-        rs = [r for r in range(n) if r != rank and rank in halves(r)[h]]
-        cnt["r_f%d" % h] = sum(len(masks(r, halves(r)[h])[rank]) for r in rs)
-        groups.append(rs)
+    early = [r for r in others(rank) if rank in halves(r)[0]]
+    late = [r for r in others(rank) if rank in halves(r)[1]]
+    late = [r for r in late if r in on] + [r for r in late if r not in on]
+    for h, rs in enumerate([early, late]):
+        for r in rs:
+            cnt["r_f%d" % r] = len(masks(r, halves(r)[h])[rank])
 
     need("v", "t_w", "i_kw")
     fin(V.tensor_tensor(T.wout[:], T.pm[0:1, 300:308], T.kw[:], A.add), "v_w")
@@ -337,14 +364,11 @@ def rank_program(g, core, T, topo):
 
     need("t", "v_e1")
     k = korder.index(rank)
-    E.matmul(T.pc[:, 0:32], T.idb[:], T.sendf[:, 32 * k:32 * k + 32], True, False)
-    for h in range(2):
-        need("t", "r_f%d" % h)
-        for i, r in enumerate(groups[h]):
-            last = h == 1 and i == len(groups[h]) - 1
-            ins = E.matmul(T.pc[:, 0:32], T.idb[:], T.landf[:, 32 * r:32 * r + 32], False, last)
-            if last:
-                fin(ins, "t_y")
+    E.matmul(T.pc[:, 0:32], T.idh[:], T.sendf[:, 32 * k:32 * k + 32], True, False)
+    for i, r in enumerate(early + late):
+        need("t", "r_f%d" % r)
+        ins = E.matmul(T.pc[:, 0:32], T.idh[:], T.landf[:, 32 * r:32 * r + 32], False, i == n - 2)
+    fin(ins, "t_y")
     need("v", "t_y")
     fin(V.tensor_copy(T.yout[:], T.pc[:, 0:32]), "v_y")
     need("y", "v_y")

@@ -3,41 +3,43 @@ from concourse.mybir import AluOpType, AxisListType, ActivationFunctionType
 
 ZC = 510
 ZL = 16 * ZC
-A1, A2 = 236, 292
+Z1, Z2, Z3 = 156, 246, 304
+ZG, ZV = 318, 414
 
 F32, B16, H16, I32, U16 = "float32", "bfloat16", "float16", "int32", "uint16"
 SCRATCH = {
     "pin": ("sbuf", [128, 8, 64], I32), "pf": ("sbuf", [128, 4, 8, 16], H16),
     "posi": ("sbuf", [8, 2], I32), "posb": ("sbuf", [8, 2], B16), "posf": ("sbuf", [8, 2], F32),
     "feat": ("sbuf", [8, 128], B16), "gsel": ("sbuf", [8, 128], F32), "sel8": ("sbuf", [8, 128], B16),
-    "rrow": ("sbuf", [1, 128], B16), "trow": ("sbuf", [1, 128], B16), "cgt": ("sbuf", [16, 128], F32),
-    "kw": ("sbuf", [1, 8], F32), "wout": ("sbuf", [1, 8], F32),
+    "rrow": ("sbuf", [1, 128], B16), "trow": ("sbuf", [1, 128], B16), "cgt": ("sbuf", [16, 128], H16),
+    "kw": ("sbuf", [1, 8], F32), "wout": ("sbuf", [1, 8], F32), "yout": ("sbuf", [32, 128], F32),
 }
 for _nm, _w, _t in [
-        ("trs", 2048, B16), ("nat", 512, F32), ("off", 512, U16), ("zed", ZL, B16), ("ints", 4, I32), ("cols", 4, F32),
-        ("col8", 1, F32), ("cu", 144, F32), ("cm8", 128, F32), ("aj", 256, F32), ("bj", 256, F32),
-        ("bsel", 8, H16), ("qs", 144, B16), ("idh", 128, H16), ("idf", 128, F32), ("em", 128, F32),
-        ("zero", 32, F32), ("dfw", 32, F32), ("kcol", 128, F32), ("ccol", 1, F32), ("coef", 128, F32),
-        ("gee", 128, B16), ("kyi", 128, F32), ("kysq", 128, F32), ("cst", 128, F32), ("lh4", 128, B16), ("lhw", 1, B16),
-        ("neg", 2, F32), ("b8", 2, F32), ("b8s", 2, F32), ("yy", 256, F32), ("ss", 256, I32),
-        ("rj", 256, I32), ("mask", 256, F32), ("dxc", 1, F32), ("rx2", 1, F32), ("dyc", 16, F32), ("cidx", 16, U16),
-        ("yg", 256, H16), ("off2", 16, U16), ("cg", 256, B16), ("sendc", 32, H16), ("landc", 256, H16), ("sq", 32, F32),
-        ("cmx", 32, F32), ("uu", 32, F32), ("ud", 32, F32), ("ff", 1, F32), ("rhs", 128, B16), ("lst", 128, U16),
-        ("fg", 2048, B16), ("sendf", 256, H16), ("landf", 256, H16), ("yout", 32, F32)]:
+        ("row", 512, I32), ("trs", 2048, B16), ("off", 512, U16), ("zed", ZL, B16), ("ints", 4, I32), ("cols", 4, F32),
+        ("cmid", 1, F32), ("cu", 144, F32), ("aj", 256, F32), ("bj", 256, F32), ("bsel", 8, H16), ("qs", 48, B16),
+        ("idh", 128, H16), ("idf", 128, F32), ("one", 128, F32), ("em0", 128, F32), ("em", 128, F32),
+        ("dfw", 32, F32), ("kcol", 128, B16), ("ccol", 1, F32), ("coef", 128, B16),
+        ("gee", 128, B16), ("kyi", 128, B16), ("kysq", 128, F32), ("lh4", 128, B16), ("lhw", 1, B16),
+        ("neg", 2, F32), ("yy", 256, F32), ("ss", 256, F32), ("rj", 256, F32), ("mask", 256, F32), ("wcol", 1, F32),
+        ("dxc", 1, F32), ("rx2", 1, F32), ("rxo", 1, F32), ("dyc", 16, F32), ("sl", 16, I32), ("ci", 16, I32),
+        ("cidx", 16, U16), ("yg", 256, H16), ("off2", 16, U16), ("cg", 256, B16), ("sendc", 32, H16),
+        ("landc", 256, H16), ("sq", 32, F32), ("mx", 1, F32), ("uu", 32, F32), ("ff", 32, F32), ("rhs", 128, B16),
+        ("lst", 128, U16), ("fg", 2048, B16), ("sendf", 256, H16), ("landf", 256, H16)]:
     SCRATCH[_nm] = ("sbuf", [128, _w], _t)
 for _nm in ["pt", "po", "pc", "pe", "ps", "pf0", "pf1", "pm"]:
     SCRATCH[_nm] = ("psum", [128, 512], F32)
-SEMAPHORES = ["s_pos", "s_tau", "s_tr", "s_w", "s_y",
-              "i_p", "i_sel", "i_aj", "i_bj", "i_u", "i_m8", "i_d", "i_k", "i_c", "i_ky", "i_rr", "i_kw",
-              "m_z", "m_d0", "m_d1", "m_co", "m_c2", "m_lw0", "m_lw1", "m_ft", "m_tr0", "m_tr1",
-              "v_int", "v_col", "v_c2", "v_sel", "v_bs", "v_qs", "v_id", "v_idh", "v_em", "v_km", "v_g", "v_posb",
-              "v_posf", "v_feat", "v_cidx", "v_ss", "v_rj", "v_mask", "v_pf0", "v_pf1", "v_pf2", "v_pf3", "v_yg",
-              "v_off", "v_off2", "v_cg", "v_sendc", "v_z", "v_cm", "v_u", "v_ud", "v_f", "v_rhs", "v_l0", "v_l1",
-              "v_g0", "v_g1", "v_g2", "v_g3", "v_e0", "v_e1", "v_w", "v_y",
-              "a_neg", "a_xx", "a_dc", "a_rx", "a_ky", "a_cst", "a_n", "a_lh4", "a_cgt", "a_cg", "a_z", "a_sq",
-              "a_g0", "a_g1", "a_g2", "a_g3",
-              "t_pos", "t_t0", "t_t1", "t_t2", "t_t3", "t_o1", "t_off", "t_c", "t_lh4", "t_sum", "t_e", "t_s", "t_w",
-              "t_f0", "t_f1", "t_y", "l_c", "l_f"] + ["r_c%d" % _i for _i in range(8)] + ["r_f%d" % _i for _i in range(8)]
+SEMAPHORES = ["s_pos", "s_row", "s_tau", "s_tr", "s_w", "s_y",
+              "i_p", "i_sel", "i_aj", "i_bj", "i_u", "i_k", "i_ky", "i_c", "i_rr", "i_kw", "i_e0", "i_em", "i_id",
+              "m_lw0", "m_lw1", "m_ft", "m_tr0", "m_tr1",
+              "v_int", "v_col", "v_cmid", "v_wcol", "v_sel", "v_bs", "v_qs", "v_idh", "v_km", "v_g", "v_posb",
+              "v_posf", "v_feat", "v_sl", "v_ci", "v_cidx", "v_ss0", "v_ss1", "v_pf0", "v_pf2",
+              "v_yg", "v_cgt", "v_off0", "v_off1", "v_off2", "v_cg", "v_sendc", "v_z", "v_mx", "v_u", "v_f", "v_rhs",
+              "v_l0", "v_l1", "v_e0", "v_e1", "v_w", "v_y",
+              "a_one", "a_d", "a_d1", "a_neg", "a_xx0", "a_xx1", "a_dc", "a_rx", "a_rxo", "a_t0", "a_t1", "a_m",
+              "a_ky", "a_lh4", "a_z", "a_sq",
+              "t_pos", "t_n", "t_o1", "t_off", "t_c", "t_lh4", "t_sum", "t_e", "t_s", "t_w",
+              "t_f0", "t_f1", "t_y", "l_t", "l_c", "l_f", "r_t"] + ["p%d" % _i for _i in range(8)] \
+    + ["r_c%d" % _i for _i in range(8)] + ["r_f%d" % _i for _i in range(8)]
 
 
 def rank_program(g, core, T, topo):
@@ -107,145 +109,181 @@ def rank_program(g, core, T, topo):
         return DstId(rid=rid, pnc=pid)
 
     korder = order(rank)
+    h0 = korder[0] // half
+    h1 = korder[half] // half
+    hs = [(korder[half * h], slice(64 * h, 64 * h + 64)) for h in range(2)]
+    off, oe, on, ne = coarse_masks(rank)
 
     fin(Y.dma_start(T.posi[:], T.pos[:]), "s_pos", 16)
+    fin(S.dma_start(T.row[:], T.tau[:]), "s_row", 16)
     for s in range(8):
-        q = Y if s < 3 else S
+        q = Y if s < 4 else S
         fin(q.dma_start(T.pin[:, s, :], T.tau[s:s + 1, :]), "s_tau", 16)
-    fin(S.dma_start(T.trs[:], T.tr[:]), "s_tr", 16)
+    fin(Y.dma_start(T.trs[:], T.tr[:]), "s_tr", 16)
 
     def iota(ap, pat, base, cm, name):
         fin(g.iota(ap, pat, base, cm, allow_small_or_imprecise_dtypes=True), name)
 
     fin(g.iota(T.ints[:, 0:1], [[1, 1]], 0, 1), "i_p")
     iota(T.gsel[:], [[1, 8], [0, 16]], 0, -1, "i_sel")
-    iota(T.aj[:], [[0, 16], [1, 16]], 0, 0, "i_aj")
-    iota(T.bj[:], [[1, 16], [0, 16]], 0, 0, "i_bj")
-    iota(T.cu[:], [[1, 144]], 0, 0, "i_u")
+    iota(T.cu[:], [[1, 144]], -16, 0, "i_u")
+    iota(T.aj[:], [[0, 16], [-16, 16]], 248, 0, "i_aj")
+    iota(T.bj[:], [[32, 8], [-16, 2], [0, 16]], 24, 0, "i_bj")
+    pair = [d for d in on if d // half == rank // half]
+    both = sorted(pair[:1] + [rank])
+    if rank == both[0]:
+        iota(T.kyi[:], [[32 * half * (h1 - h0), 2], [32, half], [1, 16]], 32 * half * h0, 0, "i_ky")
+    if rank == both[-1]:
+        iota(T.kcol[:], [[h1 - h0, 2], [2, half], [0, 16]], h0, 0, "i_k")
+    if pair:
+        tab, nm = (T.kyi, "i_ky") if rank == both[0] else (T.kcol, "i_k")
+        need("g", nm)
+        g.remote_dma_fused([RemoteDMATransfer(dst_ids=[dst(pair[0])], dma_engine_mask=bits(es), remote_sem=T.sem["r_t"],
+                                              srcs=[tab[:, c:c + 64]], dsts=[tab[:, c:c + 64]])
+                            for es, c in ((oe, 0), (ne, 64))], local_sem=T.sem["l_t"])
+        cnt["l_t"] = len(oe) + len(ne)
+    cnt["r_t"] = cnt.get("l_t", 0)
+    cnt.setdefault("i_ky", 0)
+    cnt.setdefault("i_k", 0)
     iota(T.rrow[:], [[0, 8], [1, 16]], 0, 0, "i_rr")
-    iota(T.cm8[:], [[0, 16], [1, 8]], 0, 0, "i_m8")
-    hs = [(korder[half * h], slice(64 * h, 64 * h + 64)) for h in range(2)]
-    for k0, c in hs:
-        iota(T.kyi[:, c], [[2, 8], [32, 4], [1, 2]], 32 * k0, 0, "i_ky")
-    for k0, c in hs:
-        iota(T.kcol[:, c], [[0, 8], [1, 4], [0, 2]], k0, 0, "i_k")
-    for k0, c in hs:
-        iota(T.coef[:, c], [[2, 8], [32, 4], [1, 2]], 8 + 32 * k0, 0, "i_c")
-    iota(T.dfw[0:32, :], [[0, 2], [2, 16]], 1, 0, "i_d")
-    iota(T.kw[:], [[32, 8]], 0, 0, "i_kw")
 
     def ms(ap, x, name):
         fin(V.memset(ap, x), name)
 
+    def eq(out, in0, col, name):
+        fin(V.tensor_scalar(out, in0, col, None, A.is_equal), name)
+
     ms(T.feat[:], 1.0, "m_ft")
     ms(T.trow[:], 0.0, "m_tr0")
-    ms(T.ccol[:], 8.0, "m_co")
-    ms(T.dfw[32:64, :], 1.0, "m_d0")
-    ms(T.dfw[64:128, :], 0.0, "m_d0")
-    ms(T.lhw[:], 0.0, "m_lw0")
-    ms(T.zero[:], 0.0, "m_z")
     need("v", "i_p")
-    fin(V.tensor_scalar(T.ints[:, 1:2], T.ints[:, 0:1], 15, None, A.bitwise_and), "v_int")
-    fin(V.tensor_scalar(T.ints[:, 2:3], T.ints[:, 0:1], 7, None, A.bitwise_and), "v_int")
-    fin(V.tensor_scalar(T.ints[:, 3:4], T.ints[:, 0:1], 112, None, A.bitwise_and), "v_int")
-    need("v", "m_d0", "m_lw0", "m_tr0", "m_co")
-    ms(T.trow[:, 32:64], 1.0, "m_tr1")
-    ms(T.ccol[0:32, :], 64.0, "m_c2")
-    need("v", "v_int")
-    fin(V.tensor_copy(T.cols[:], T.ints[:]), "v_col")
+    for i, b in ((1, 15), (2, 7), (3, 112)):
+        fin(V.tensor_scalar(T.ints[:, i:i + 1], T.ints[:, 0:1], b, None, A.bitwise_and), "v_int")
     need("v", "i_sel")
     fin(V.tensor_scalar(T.sel8[:], T.gsel[:], 0.0, None, A.is_equal), "v_sel")
+    need("v", "v_int", "m_tr0")
+    fin(V.tensor_copy(T.cols[:], T.ints[:]), "v_col")
+    ms(T.trow[:, 32:64], 1.0, "m_tr1")
+    ms(T.lhw[:], 0.0, "m_lw0")
     need("v", "v_col")
-    fin(V.tensor_scalar(T.col8[:], T.cols[:, 1:2], 8.0, 7.0, A.mult, A.add), "v_c2")
-    ms(T.dfw[32:64, 15:16], -15.0, "m_d1")
-    ms(T.dfw[64:128, 15:16], 1.0, "m_d1")
+    fin(V.tensor_scalar(T.cmid[:], T.cols[:, 1:2], -16.0, 248.0, A.mult, A.add), "v_cmid")
+    fin(V.tensor_scalar(T.wcol[:], T.cols[:, 1:2], -2.0, -4095.5 / 4096, A.mult, A.add), "v_wcol")
+    need("v", "i_u")
+    eq(T.bsel[:], T.cu[:, 16:144:16], T.cols[:, 3:4], "v_bs")
+    eq(T.idh[:], T.cu[:, 16:144], T.cols[:, 0:1], "v_idh")
+    eq(T.qs[:], T.cu[:, 0:48], T.cols[:, 1:2], "v_qs")
+    need("v", "m_lw0")
     ms(T.lhw[32:64, :], 1.0 / 32, "m_lw1")
     ms(T.lhw[96:128, :], 0.5, "m_lw1")
+
+    def table(ap, x, k, b, name):
+        fin(S.activation(ap, x, F.Copy, bias=b, scale=k), name)
+
+    need("s", "i_u")
+    table(T.one[:], T.cu[:, 0:128], 0.0, 1.0, "a_one")
+    for c in (0, 16):
+        table(T.dfw[0:32, c:c + 16], T.cu[0:32, 16:32], -2.0, 29.0, "a_d")
+    table(T.dfw[32:64, :], T.cu[32:64, 0:32], 0.0, 1.0, "a_d")
+    table(T.dfw[64:128, :], T.cu[64:128, 0:32], 0.0, 0.0, "a_d")
+    table(T.ccol[:], T.cu[:, 0:1], 0.0, 8.0, "a_d")
+    need("s", "a_d")
+    for c, p0, p1, x in ((15, 0, 32, -225.0), (15, 32, 64, -15.0), (15, 64, 128, 1.0), (31, 0, 64, 0.0)):
+        table(T.dfw[p0:p1, c:c + 1], T.cu[p0:p1, 0:1], 0.0, x, "a_d1")
+    table(T.ccol[0:32, :], T.cu[0:32, 0:1], 0.0, 64.0, "a_d1")
+    need("g", "a_one")
+    fin(g.affine_select(T.em0[:], T.one[:], [[0, 16], [-16, 8]], A.is_ge, 0.0, 0, 1), "i_e0")
+    need("g", "i_e0")
+    fin(g.affine_select(T.em[:], T.em0[:], [[0, 16], [16, 8]], A.is_ge, 0.0, 15, -1), "i_em")
+
     need("v", "s_pos")
     fin(V.tensor_copy(T.posb[:], T.posi[:]), "v_posb")
     fin(V.tensor_copy(T.posf[:], T.posi[:]), "v_posf")
     need("t", "v_sel", "v_posb")
     fin(E.matmul(T.pm[:, 0:2], T.sel8[:], T.posb[:], True, True), "t_pos")
-    need("v", "v_c2", "i_u")
-    fin(V.tensor_scalar(T.idh[:], T.cu[:, 0:128], T.cols[:, 0:1], None, A.is_equal), "v_idh")
-    need("v", "v_posf", "m_ft")
-    fin(V.tensor_scalar(T.feat[:, 32:64], T.feat[:, 0:32], T.posf[:, 0:1], -1.0, A.mult, A.mult), "v_feat")
-    fin(V.tensor_scalar(T.feat[:, 96:128], T.feat[:, 0:32], T.posf[:, 1:2], -1.0, A.mult, A.mult), "v_feat")
-    fin(V.tensor_scalar(T.idf[:], T.cu[:, 0:128], T.cols[:, 0:1], None, A.is_equal), "v_id")
     need("s", "t_pos")
-    fin(S.activation(T.b8[:], T.pm[:, 0:2], F.Copy, bias=8.0, scale=-1.0), "a_neg")
-    fin(S.activation(T.b8s[:], T.pm[:, 0:2], F.Copy, bias=0.5, scale=-0.0625), "a_neg")
     fin(S.activation(T.neg[:], T.pm[:, 0:2], F.Copy, scale=-1.0), "a_neg")
-    need("s", "a_neg", "i_aj", "i_bj", "v_col", "i_u")
-    fin(S.activation(T.pf1[:, 0:256], T.aj[:], F.Square, bias=T.b8[:, 0:1], scale=16.0), "a_xx")
-    fin(S.activation(T.yy[:], T.bj[:], F.Square, bias=T.b8[:, 1:2], scale=16.0), "a_xx")
-    fin(S.activation(T.dyc[:], T.cu[:, 0:16], F.Square, bias=T.b8s[:, 1:2]), "a_dc")
-    fin(S.activation(T.dxc[:], T.cols[:, 1:2], F.Square, bias=T.b8s[:, 0:1]), "a_dc")
+    need("s", "a_neg", "i_aj", "i_bj", "v_cmid", "v_col")
+    for h in range(2):
+        c = slice(128 * h, 128 * h + 128)
+        fin(S.activation(T["pf%d" % h][:, 0:128], T.aj[:, c], F.Square, bias=T.neg[:, 0:1]), "a_xx%d" % h)
+        fin(S.activation(T.yy[:, c], T.bj[:, c], F.Square, bias=T.neg[:, 1:2]), "a_xx%d" % h)
+        if h == 0:
+            fin(S.activation(T.dyc[:], T.bj[:, 0:256:16], F.Square, bias=T.neg[:, 1:2]), "a_dc")
+            fin(S.activation(T.dxc[:], T.cmid[:], F.Square, bias=T.neg[:, 0:1]), "a_dc")
     fin(S.activation(T.rx2[:], T.cols[:, 1:2], F.Square, bias=T.neg[:, 0:1]), "a_rx")
-    need("v", "a_xx")
-    fin(V.tensor_tensor(T.ss[:], T.pf1[:, 0:256], T.yy[:], A.add), "v_ss")
+    for h in range(2):
+        c = slice(128 * h, 128 * h + 128)
+        need("v", "a_xx%d" % h)
+        fin(V.tensor_tensor(T.ss[:, c], T["pf%d" % h][:, 0:128], T.yy[:, c], A.add), "v_ss%d" % h)
+        if h == 0:
+            need("v", "a_dc")
+            fin(V.tensor_scalar(T.sl[:], T.dyc[:], T.dxc[:, 0:1], None, A.add), "v_sl")
+            need("v", "v_sl")
+            fin(V.tensor_scalar(T.ci[:], T.sl[:], 4, 511, A.arith_shift_right, A.bitwise_and), "v_ci")
+            need("v", "v_ci")
+            fin(V.tensor_copy(T.cidx[:], T.ci[:]), "v_cidx")
+    for h in range(2):
+        c = slice(128 * h, 128 * h + 128)
+        need("s", "v_ss%d" % h, "v_wcol")
+        fin(S.activation(T.rj[:, c], T.ss[:, c], F.Square, bias=T.wcol[:, 0:1], scale=1.0 / 4096), "a_t%d" % h)
+    for h in range(2):
+        c = slice(128 * h, 128 * h + 128)
+        need("s", "a_t%d" % h)
+        fin(S.activation(T.mask[:, c], T.rj[:, c], F.Relu, bias=1e7, scale=-1e7), "a_m")
+    need("s", "a_rx")
+    fin(S.activation(T.rxo[:], T.rx2[:], F.Copy, bias=-15.0 / 32, scale=0.0625), "a_rxo")
 
-    def piece(cb):
-        fin(V.tensor_copy(T.pf[:, cb, :, :], T.pin[:, :, 16 * cb:16 * cb + 16]), "v_pf%d" % cb)
-        bank = T[["pt", "po", "pc", "pe"][cb]]
+    def turn(cb):
+        need("v", "s_tau")
+        for i in (cb, cb + 1):
+            fin(V.tensor_copy(T.pf[:, i, :, :], T.pin[:, :, 16 * i:16 * i + 16]), "v_pf%d" % cb)
         need("t", "v_pf%d" % cb, "v_idh")
-        fin(E.matmul(bank[:, 0:128], T.pf[:, cb, :, :], T.idh[:], True, True), "t_t%d" % cb)
-        need("s", "t_t%d" % cb)
-        fin(S.activation(T.nat[:, cb::4], bank[:, 0:128], F.Copy), "a_n")
+        for i in (cb, cb + 1):
+            ins = E.matmul(T.pe[:, i::4], T.pf[:, i, :, :], T.idh[:], True, True)
+        if cb == 2:
+            fin(ins, "t_n")
 
-    need("v", "s_tau")
-    piece(0)
-    piece(1)
-    need("v", "v_ss")
-    fin(V.tensor_scalar(T.rj[:], T.ss[:], 4, 15, A.arith_shift_right, A.bitwise_and), "v_rj")
-    piece(2)
-    piece(3)
-    need("v", "v_rj")
-    fin(V.tensor_scalar(T.mask[:], T.rj[:], T.cols[:, 1:2], None, A.is_equal), "v_mask")
-    need("v", "a_dc")
-    fin(V.tensor_scalar(T.cidx[:], T.dyc[:], T.dxc[:, 0:1], -255.0 / 512, A.add, A.add), "v_cidx")
-    fin(V.tensor_scalar(T.bsel[:], T.cu[:, 0:128:16], T.cols[:, 3:4], None, A.is_equal), "v_bs")
-    fin(V.tensor_scalar(T.qs[:], T.cu[:], T.col8[:, 0:1], None, A.is_equal), "v_qs")
-    need("t", "v_feat", "m_ft", "m_tr1", "i_rr", "a_neg")
-    E.matmul(T.pm[:, 128:256], T.feat[:], T.sel8[:], True, False)
-    fin(E.matmul(T.pm[:, 128:256], T.trow[:], T.rrow[:], False, True), "t_lh4")
-    need("s", "t_lh4")
-    fin(S.activation(T.lh4[:], T.pm[:, 128:256], F.Copy), "a_lh4")
-    need("v", "a_n", "v_cidx", "v_mask")
-    fin(V.tensor_tensor(T.yg[:], T.nat[:, 0:512].indirect(T.cidx[:, 0:16]), T.mask[:], A.mult), "v_yg")
-    need("t", "v_yg", "v_bs", "a_n")
+    turn(0)
+    turn(2)
+    need("v", "v_cidx", "a_m", "s_row")
+    fin(V.tensor_tensor(T.yg[:], T.row[:, 0:512].indirect(T.cidx[:, 0:16]), T.mask[:], A.min), "v_yg")
+    need("t", "v_yg", "v_bs")
     for r in range(16):
         ins = E.matmul(T.po[0:16, r:128:16], T.yg[:, r::16], T.bsel[:], True, True)
     fin(ins, "t_o1")
-    need("s", "t_o1")
-    fin(S.activation(T.cgt[:], T.po[0:16, 0:128], F.Copy), "a_cgt")
-    need("t", "a_cgt", "v_id")
-    fin(E.matmul(T.pt[:, 0:16], T.cgt[:], T.idf[0:16, 0:16], True, True), "t_off")
-    need("s", "i_ky", "a_rx")
-    fin(S.activation(T.kysq[:], T.kyi[:], F.Square, bias=T.neg[:, 1:2]), "a_ky")
-    need("s", "a_ky")
-    fin(S.activation(T.cst[:], T.kysq[:], F.Identity, bias=T.rx2[:, 0:1]), "a_cst")
-    fin(V.tensor_copy(T.off[:], T.nat[:]), "v_off")
+    need("v", "t_n")
+    fin(V.tensor_copy(T.off[:, 0:256], T.pe[:, 0:256]), "v_off0")
+    need("v", "t_o1")
+    fin(V.tensor_copy(T.cgt[:], T.po[0:16, 0:128]), "v_cgt")
+    need("t", "v_cgt", "v_idh")
+    fin(E.matmul(T.pt[:, 0:16], T.cgt[:], T.idh[0:16, 0:16], True, True), "t_off")
+    fin(V.tensor_copy(T.off[:, 256:512], T.pe[:, 256:512]), "v_off1")
     need("v", "t_off")
     fin(V.tensor_copy(T.off2[:], T.pt[:, 0:16]), "v_off2")
     need("v", "v_off2", "s_tr")
-    fin(V.tensor_copy(T.cg[:, 0:128], T.trs[:, 0:2048].indirect(T.off2[:, 0:8])), "v_cg")
-    need("s", "v_off2", "s_tr")
-    fin(S.activation(T.cg[:, 128:256], T.trs[:, 0:2048].indirect(T.off2[:, 8:16]), F.Copy), "a_cg")
+    fin(V.tensor_copy(T.cg[:], T.trs[:, 0:2048].indirect(T.off2[:])), "v_cg")
     need("t", "v_qs", "v_cg")
-    for b in range(8):
-        if b == 4:
-            need("t", "a_cg")
-        ins = E.matmul(T.pc[:, 0:32], T.qs[:, 7 - b:135 - b], T.cg[:, 32 * b:32 * b + 32], b == 0, b == 7)
-        if b == 7:
-            fin(ins, "t_c")
-    need("v", "i_m8")
-    fin(V.tensor_scalar(T.em[:], T.cm8[:], T.cols[:, 2:3], None, A.is_equal), "v_em")
-    need("v", "i_k", "m_c2")
-    fin(V.tensor_scalar(T.gee[:], T.kcol[:], T.cols[:, 2:3], T.ccol[:, 0:1], A.is_equal, A.mult), "v_km")
+    for b in range(4):
+        for h in range(2):
+            c = 128 * h + 32 * b
+            ins = E.matmul(T.pc[32 * b:32 * b + 32, 0:32], T.qs[:, 16 - 16 * h:48 - 16 * h], T.cg[:, c:c + 32], h == 0, h == 1)
+    fin(ins, "t_c")
+
+    def zs(a, b):
+        need("s", "v_off0", "s_tr")
+        if b > 256:
+            need("s", "v_off1")
+        fin(S.activation(T.zed[:, 16 * a:16 * b], T.trs[:, 0:2048].indirect(T.off[:, a:b]), F.Copy), "a_z")
+
+    def zv(a, b):
+        need("v", "v_off0", "v_off1", "s_tr")
+        fin(V.tensor_copy(T.zed[:, 16 * a:16 * b], T.trs[:, 0:2048].indirect(T.off[:, a:b])), "v_z")
+
+    zv(Z3, ZG)
     need("v", "t_c")
     fin(V.tensor_copy(T.sendc[:], T.pc[:, 0:32]), "v_sendc")
-    off, oe, on, ne = coarse_masks(rank)
+    need("v", "v_posf", "m_ft")
+    fin(V.tensor_scalar(T.feat[:, 32:64], T.feat[:, 0:32], T.posf[:, 0:1], -1.0, A.mult, A.mult), "v_feat")
+    fin(V.tensor_scalar(T.feat[:, 96:128], T.feat[:, 0:32], T.posf[:, 1:2], -1.0, A.mult, A.mult), "v_feat")
     mine = slice(32 * rank, 32 * rank + 32)
     rc = T.sem["r_c%d" % rank]
     tr = [RemoteDMATransfer(dst_ids=[dst(d) for d in off], dma_engine_mask=bits(oe), remote_sem=rc,
@@ -259,83 +297,89 @@ def rank_program(g, core, T, topo):
     for r in others(rank):
         o, e1, o2, e2 = coarse_masks(r)
         cnt["r_c%d" % r] = len(e1) if rank in o else len(e2)
+    iota(T.coef[:], [[32 * half * (h1 - h0), 2], [32, half], [1, 16]], 8 + 32 * half * h0, 0, "i_c")
+    fin(g.affine_select(T.idf[:], T.one[:], [[-1, 128]], A.is_equal, 0.0, 0, 1), "i_id")
+    iota(T.kw[:], [[32, 8]], 0, 0, "i_kw")
 
-    need("s", "v_off")
-    fin(S.activation(T.zed[:, 0:16 * A1], T.trs[:, 0:2048].indirect(T.off[:, 0:A1]), F.Copy), "a_z")
-    need("t", "v_id", "a_cst")
-    E.matmul(T.ps[:, 0:128], T.idf[:], T.cst[:], True, False)
-    need("v", "v_km", "i_c", "i_d")
+    zs(0, Z1)
+    need("t", "v_feat", "m_ft", "m_tr1", "i_rr", "a_neg")
+    E.matmul(T.pm[:, 128:256], T.feat[:], T.sel8[:], True, False)
+    fin(E.matmul(T.pm[:, 128:256], T.trow[:], T.rrow[:], False, True), "t_lh4")
+    need("s", "t_lh4")
+    fin(S.activation(T.lh4[:], T.pm[:, 128:256], F.Copy), "a_lh4")
+    need("s", "i_ky", "r_t")
+    fin(S.activation(T.kysq[:], T.kyi[:], F.Square, bias=T.neg[:, 1:2]), "a_ky")
+    zs(Z1, Z2)
+    zv(ZG, ZV)
+    need("v", "i_k", "r_t", "a_d1")
+    fin(V.tensor_scalar(T.gee[:], T.kcol[:], T.cols[:, 2:3], T.ccol[:, 0:1], A.is_equal, A.mult), "v_km")
+    need("v", "v_km", "i_c")
     fin(V.tensor_tensor(T.gee[64:96, :], T.gee[64:96, :], T.coef[64:96, :], A.mult), "v_g")
-    ms(T.dfw[0:32, 15:16], -225.0, "m_d1")
-    need("v", "v_off", "s_tr")
-    fin(V.tensor_copy(T.zed[:, 16 * A2:ZL], T.trs[:, 0:2048].indirect(T.off[:, A2:ZC])), "v_z")
+    zv(ZV, ZC)
 
-    need("t", "v_sendc")
+    need("t", "v_off0", "v_off1", "v_sendc")
     E.matmul(T.pe[:, 0:32], T.idh[:], T.sendc[:], True, False)
     for i, r in enumerate([r for r in others(rank) if r in on] + [r for r in others(rank) if r not in on]):
         need("t", "r_c%d" % r)
         ins = E.matmul(T.pe[:, 0:32], T.idh[:], T.landc[:, 32 * r:32 * r + 32], False, i == n - 2)
-        if i == n - 2:
-            fin(ins, "t_sum")
+    fin(ins, "t_sum")
     need("s", "t_sum")
     fin(S.activation(T.sq[:], T.pe[:, 0:32], F.Square), "a_sq")
-    need("t", "a_sq", "v_em")
-    fin(S.activation(T.zed[:, 16 * A1:16 * A2], T.trs[:, 0:2048].indirect(T.off[:, A1:A2]), F.Copy), "a_z")
+    need("t", "a_sq", "i_em")
+    zs(Z2, Z3)
     fin(E.matmul(T.pe[:, 64:96], T.em[:], T.sq[:], True, True), "t_e")
-    need("v", "t_e", "m_z")
-    fin(V.tensor_tensor_scan(T.cmx[:], T.pe[:, 64:96], T.zero[:], 0.0, A.max, A.max), "v_cm")
-    need("v", "v_cm")
-    fin(V.tensor_scalar(T.uu[:], T.cmx[:], T.cmx[:, 31:32], None, A.is_lt), "v_u")
-    need("v", "v_u", "m_d1")
-    fin(V.tensor_tensor(T.ud[:], T.uu[:], T.dfw[:], A.mult), "v_ud")
-    need("v", "v_ud")
-    fin(V.tensor_reduce(T.ff[:], T.ud[:], AxisListType.X, A.add), "v_f")
+    need("t", "i_id", "a_ky")
+    E.matmul(T.ps[:, 0:128], T.idf[:], T.kysq[:], True, False)
+    need("v", "t_e")
+    fin(V.tensor_reduce(T.mx[:], T.pe[:, 64:96], AxisListType.X, A.max), "v_mx")
+    need("v", "v_mx")
+    fin(V.tensor_scalar(T.uu[:], T.pe[:, 64:96], T.mx[:, 0:1], None, A.is_lt), "v_u")
+    need("v", "v_u", "a_d1")
+    fin(V.tensor_tensor_scan(T.ff[:], T.uu[:], T.dfw[:], 0.0, A.mult, A.add), "v_f")
     need("v", "v_f", "v_g")
-    fin(V.tensor_scalar(T.rhs[:], T.gee[:], T.ff[:, 0:1], None, A.mult), "v_rhs")
+    fin(V.tensor_scalar(T.rhs[:], T.gee[:], T.ff[:, 31:32], None, A.mult), "v_rhs")
     need("t", "v_rhs", "a_lh4")
     fin(E.matmul(T.ps[:, 0:128], T.lh4[:], T.rhs[:], False, True), "t_s")
     need("t", "m_lw1")
     for k0, c in hs:
-        fin(E.matmul(T.pm[0:1, 300 + k0:304 + k0], T.lhw[:], T.rhs[:, c.start:c.start + 8:2], True, True), "t_w")
-    need("v", "t_s")
+        fin(E.matmul(T.pm[0:1, 300 + k0:304 + k0], T.lhw[:], T.rhs[:, c.start:c.stop:16], True, True), "t_w")
+    need("v", "t_s", "a_rxo")
     for h, (k0, c) in enumerate(hs):
-        fin(V.tensor_scalar(T.lst[:, c], T.ps[:, c], 0.0625, -15.0 / 32, A.mult, A.add), "v_l%d" % h)
+        fin(V.tensor_scalar(T.lst[:, c], T.ps[:, c], 0.0625, T.rxo[:, 0:1], A.mult, A.add), "v_l%d" % h)
 
     need("v", "v_z", "a_z")
     need("s", "v_z", "a_z")
 
-    def pick(q, h, j):
-        lo = 64 * h + 8 * j
-        o = T.fg[:, 16 * lo:16 * lo + 256]
-        w = T.zed[:, 0:ZL].indirect(T.lst[:, lo:lo + 16])
-        need(q, "v_l%d" % h)
+    def pick(q, i):
+        o = T.fg[:, 256 * i:256 * i + 256]
+        w = T.zed[:, 0:ZL].indirect(T.lst[:, 16 * i:16 * i + 16])
+        need(q, "v_l%d" % (i // half))
         if q == "s":
-            fin(S.activation(o, w, F.Copy), "a_g%d" % (2 * h + j // 2))
+            fin(S.activation(o, w, F.Copy), "p%d" % i)
         else:
-            fin(V.tensor_copy(o, w), "v_g%d" % (2 * h + j // 2 - 2))
+            fin(V.tensor_copy(o, w), "p%d" % i)
 
     def add_up(h):
-        acc = T["pf%d" % h]
-        for i, j in enumerate([0, 4, 2, 6]):
-            need("t", ("a_g%d" % (2 * h + j // 2)) if j < 4 else ("v_g%d" % (2 * h + j // 2 - 2)))
-            for jj in (j, j + 1):
-                o = 1024 * h + 128 * jj
-                ins = E.matmul(acc[:, 0:128], T.qs[:, 7 - jj:135 - jj], T.fg[:, o:o + 128], i == 0 and jj == j, i == 3 and jj > j)
+        for i in [half * h + x for x in (2, 0, 3, 1)]:
+            need("t", "p%d" % i)
+            for u in range(2):
+                c = 32 * (i - half * h) + u
+                ins = E.matmul(T["pf%d" % h][:, c:c + 31:2], T.fg[:, 256 * i + 128 * u:256 * i + 128 * u + 128],
+                               T.qs[:, 16:32], True, True)
         fin(ins, "t_f%d" % h)
 
     def ready(h):
         need("v", "t_f%d" % h)
         fin(V.tensor_copy(T.sendf[:, 128 * h:128 * h + 128], T["pf%d" % h][:, 0:128]), "v_e%d" % h)
 
-    for h in range(2):
-        pick("s", h, 0)
-        pick("s", h, 2)
-    pick("v", 0, 4)
-    pick("v", 0, 6)
+    for i in (0, 1, 4, 5):
+        pick("s", i)
+    for i in (2, 3):
+        pick("v", i)
     add_up(0)
-    pick("v", 1, 4)
+    pick("v", 6)
     ready(0)
-    pick("v", 1, 6)
+    pick("v", 7)
     add_up(1)
     ready(1)
 
@@ -364,13 +408,13 @@ def rank_program(g, core, T, topo):
 
     need("t", "v_e1")
     k = korder.index(rank)
-    E.matmul(T.pc[:, 0:32], T.idh[:], T.sendf[:, 32 * k:32 * k + 32], True, False)
+    E.matmul(T.pc[0:32, 0:128], T.sendf[:, 32 * k:32 * k + 32], T.idh[:], True, False)
     for i, r in enumerate(early + late):
         need("t", "r_f%d" % r)
-        ins = E.matmul(T.pc[:, 0:32], T.idh[:], T.landf[:, 32 * r:32 * r + 32], False, i == n - 2)
+        ins = E.matmul(T.pc[0:32, 0:128], T.landf[:, 32 * r:32 * r + 32], T.idh[:], False, i == n - 2)
     fin(ins, "t_y")
     need("v", "t_y")
-    fin(V.tensor_copy(T.yout[:], T.pc[:, 0:32]), "v_y")
+    fin(V.tensor_copy(T.yout[:], T.pc[0:32, 0:128]), "v_y")
     need("y", "v_y")
     fin(Y.dma_start(T.y[:], T.yout[:]), "s_y", 16)
     need("y", "s_w", "s_y")

from concourse.bass import DstId, RemoteDMATransfer
from concourse.mybir import AluOpType, AxisListType, ActivationFunctionType

ZC = 510
ZL = 16 * ZC
Z1, Z2, Z3 = 156, 246, 304
ZG, ZV = 318, 414

F32, B16, H16, I32, U16 = "float32", "bfloat16", "float16", "int32", "uint16"
SCRATCH = {
    "pin": ("sbuf", [128, 8, 64], I32), "pf": ("sbuf", [128, 4, 8, 16], H16),
    "posi": ("sbuf", [8, 2], I32), "posb": ("sbuf", [8, 2], B16), "posf": ("sbuf", [8, 2], F32),
    "feat": ("sbuf", [8, 128], B16), "gsel": ("sbuf", [8, 128], F32), "sel8": ("sbuf", [8, 128], B16),
    "rrow": ("sbuf", [1, 128], B16), "trow": ("sbuf", [1, 128], B16), "cgt": ("sbuf", [16, 128], H16),
    "kw": ("sbuf", [1, 8], F32), "wout": ("sbuf", [1, 8], F32), "yout": ("sbuf", [32, 128], F32),
}
for _nm, _w, _t in [
        ("row", 512, I32), ("trs", 2048, B16), ("off", 512, U16), ("zed", ZL, B16), ("ints", 4, I32), ("cols", 4, F32),
        ("cmid", 1, F32), ("cu", 144, F32), ("aj", 256, F32), ("bj", 256, F32), ("bsel", 8, H16), ("qs", 48, B16),
        ("idh", 128, H16), ("idf", 128, F32), ("one", 128, F32), ("em0", 128, F32), ("em", 128, F32),
        ("dfw", 32, F32), ("kcol", 128, B16), ("ccol", 1, F32), ("coef", 128, B16),
        ("gee", 128, B16), ("kyi", 128, B16), ("kysq", 128, F32), ("lh4", 128, B16), ("lhw", 1, B16),
        ("neg", 2, F32), ("yy", 256, F32), ("ss", 256, F32), ("rj", 256, F32), ("mask", 256, F32), ("wcol", 1, F32),
        ("dxc", 1, F32), ("rx2", 1, F32), ("rxo", 1, F32), ("dyc", 16, F32), ("sl", 16, I32), ("ci", 16, I32),
        ("cidx", 16, U16), ("yg", 256, H16), ("off2", 16, U16), ("cg", 256, B16), ("sendc", 32, H16),
        ("landc", 256, H16), ("sq", 32, F32), ("mx", 1, F32), ("uu", 32, F32), ("ff", 32, F32), ("rhs", 128, B16),
        ("lst", 128, U16), ("fg", 2048, B16), ("sendf", 256, H16), ("landf", 256, H16)]:
    SCRATCH[_nm] = ("sbuf", [128, _w], _t)
for _nm in ["pt", "po", "pc", "pe", "ps", "pf0", "pf1", "pm"]:
    SCRATCH[_nm] = ("psum", [128, 512], F32)
SEMAPHORES = ["s_pos", "s_row", "s_tau", "s_tr", "s_w", "s_y",
              "i_p", "i_sel", "i_aj", "i_bj", "i_u", "i_k", "i_ky", "i_c", "i_rr", "i_kw", "i_e0", "i_em", "i_id",
              "m_lw0", "m_lw1", "m_ft", "m_tr0", "m_tr1",
              "v_int", "v_col", "v_cmid", "v_wcol", "v_sel", "v_bs", "v_qs", "v_idh", "v_km", "v_g", "v_posb",
              "v_posf", "v_feat", "v_sl", "v_ci", "v_cidx", "v_ss0", "v_ss1", "v_pf0", "v_pf2",
              "v_yg", "v_cgt", "v_off0", "v_off1", "v_off2", "v_cg", "v_sendc", "v_z", "v_mx", "v_u", "v_f", "v_rhs",
              "v_l0", "v_l1", "v_e0", "v_e1", "v_w", "v_y",
              "a_one", "a_d", "a_d1", "a_neg", "a_xx0", "a_xx1", "a_dc", "a_rx", "a_rxo", "a_t0", "a_t1", "a_m",
              "a_ky", "a_lh4", "a_z", "a_sq",
              "t_pos", "t_n", "t_o1", "t_off", "t_c", "t_lh4", "t_sum", "t_e", "t_s", "t_w",
              "t_f0", "t_f1", "t_y", "l_t", "l_c", "l_f", "r_t"] + ["p%d" % _i for _i in range(8)] \
    + ["r_c%d" % _i for _i in range(8)] + ["r_f%d" % _i for _i in range(8)]


def rank_program(g, core, T, topo):
    rank = T.rank_of(core)
    if rank is None:
        return
    A, F = AluOpType, ActivationFunctionType
    cores = list(T.cores)
    n = len(cores)
    half = n // 2
    V, S, E, Y = g.vector, g.scalar, g.tensor, g.sync
    Q = {"g": g, "v": V, "s": S, "t": E, "y": Y}
    cnt, seen = {}, {}

    def fin(ins, name, k=1):
        ins.then_inc(T.sem[name], k)
        cnt[name] = cnt.get(name, 0) + k

    def need(q, *names):
        for nm in names:
            if seen.get((q, nm), 0) < cnt[nm]:
                Q[q].wait_ge(T.sem[nm], cnt[nm])
                seen[(q, nm)] = cnt[nm]

    def order(r):
        h = r // half
        return [k for hh in (1 - h, h) for k in range(half * hh, half * hh + half)]

    def bits(es):
        return sum(1 << e for e in es)

    def far(r, d):
        a, b = topo.chip(cores[r]), topo.chip(cores[d])
        return (3 if a == b else 2 if topo.same_plane(a, b) else 1 if topo.mates(a, b) else 0, r ^ d)

    def masks(r, dests):
        src = cores[r]
        off = [d for d in dests if topo.chip(cores[d]) != topo.chip(src)]
        out, taken = {}, []
        for i, d in enumerate(off):
            es = topo.engines(src, cores[d])
            w = len(es) // len(off)
            out[d] = es[i * w:i * w + w]
            taken = es
        for d in dests:
            if d not in off:
                out[d] = [e for e in topo.engines(src, cores[d]) if e not in taken][:2]
        return out

    def halves(r):
        o = order(r)
        return [d for d in o[:half] if d != r], [d for d in o[half:] if d != r]

    def others(r):
        return sorted([d for d in range(n) if d != r], key=lambda d: far(r, d))

    def coarse_masks(r):
        src = cores[r]
        off = [d for d in others(r) if topo.chip(cores[d]) != topo.chip(src)]
        on = [d for d in others(r) if d not in off]
        oe = topo.engines(src, cores[off[0]])
        ne = [e for e in topo.engines(src, cores[on[0]]) if e not in oe][:2] if on else []
        return off, oe, on, ne

    def dst(d):
        rid, pid, _ = topo.addr(cores[d])
        return DstId(rid=rid, pnc=pid)

    korder = order(rank)
    h0 = korder[0] // half
    h1 = korder[half] // half
    hs = [(korder[half * h], slice(64 * h, 64 * h + 64)) for h in range(2)]
    off, oe, on, ne = coarse_masks(rank)

    fin(Y.dma_start(T.posi[:], T.pos[:]), "s_pos", 16)
    fin(S.dma_start(T.row[:], T.tau[:]), "s_row", 16)
    for s in range(8):
        q = Y if s < 4 else S
        fin(q.dma_start(T.pin[:, s, :], T.tau[s:s + 1, :]), "s_tau", 16)
    fin(Y.dma_start(T.trs[:], T.tr[:]), "s_tr", 16)

    def iota(ap, pat, base, cm, name):
        fin(g.iota(ap, pat, base, cm, allow_small_or_imprecise_dtypes=True), name)

    fin(g.iota(T.ints[:, 0:1], [[1, 1]], 0, 1), "i_p")
    iota(T.gsel[:], [[1, 8], [0, 16]], 0, -1, "i_sel")
    iota(T.cu[:], [[1, 144]], -16, 0, "i_u")
    iota(T.aj[:], [[0, 16], [-16, 16]], 248, 0, "i_aj")
    iota(T.bj[:], [[32, 8], [-16, 2], [0, 16]], 24, 0, "i_bj")
    pair = [d for d in on if d // half == rank // half]
    both = sorted(pair[:1] + [rank])
    if rank == both[0]:
        iota(T.kyi[:], [[32 * half * (h1 - h0), 2], [32, half], [1, 16]], 32 * half * h0, 0, "i_ky")
    if rank == both[-1]:
        iota(T.kcol[:], [[h1 - h0, 2], [2, half], [0, 16]], h0, 0, "i_k")
    if pair:
        tab, nm = (T.kyi, "i_ky") if rank == both[0] else (T.kcol, "i_k")
        need("g", nm)
        g.remote_dma_fused([RemoteDMATransfer(dst_ids=[dst(pair[0])], dma_engine_mask=bits(es), remote_sem=T.sem["r_t"],
                                              srcs=[tab[:, c:c + 64]], dsts=[tab[:, c:c + 64]])
                            for es, c in ((oe, 0), (ne, 64))], local_sem=T.sem["l_t"])
        cnt["l_t"] = len(oe) + len(ne)
    cnt["r_t"] = cnt.get("l_t", 0)
    cnt.setdefault("i_ky", 0)
    cnt.setdefault("i_k", 0)
    iota(T.rrow[:], [[0, 8], [1, 16]], 0, 0, "i_rr")

    def ms(ap, x, name):
        fin(V.memset(ap, x), name)

    def eq(out, in0, col, name):
        fin(V.tensor_scalar(out, in0, col, None, A.is_equal), name)

    ms(T.feat[:], 1.0, "m_ft")
    ms(T.trow[:], 0.0, "m_tr0")
    need("v", "i_p")
    for i, b in ((1, 15), (2, 7), (3, 112)):
        fin(V.tensor_scalar(T.ints[:, i:i + 1], T.ints[:, 0:1], b, None, A.bitwise_and), "v_int")
    need("v", "i_sel")
    fin(V.tensor_scalar(T.sel8[:], T.gsel[:], 0.0, None, A.is_equal), "v_sel")
    need("v", "v_int", "m_tr0")
    fin(V.tensor_copy(T.cols[:], T.ints[:]), "v_col")
    ms(T.trow[:, 32:64], 1.0, "m_tr1")
    ms(T.lhw[:], 0.0, "m_lw0")
    need("v", "v_col")
    fin(V.tensor_scalar(T.cmid[:], T.cols[:, 1:2], -16.0, 248.0, A.mult, A.add), "v_cmid")
    fin(V.tensor_scalar(T.wcol[:], T.cols[:, 1:2], -2.0, -4095.5 / 4096, A.mult, A.add), "v_wcol")
    need("v", "i_u")
    eq(T.bsel[:], T.cu[:, 16:144:16], T.cols[:, 3:4], "v_bs")
    eq(T.idh[:], T.cu[:, 16:144], T.cols[:, 0:1], "v_idh")
    eq(T.qs[:], T.cu[:, 0:48], T.cols[:, 1:2], "v_qs")
    need("v", "m_lw0")
    ms(T.lhw[32:64, :], 1.0 / 32, "m_lw1")
    ms(T.lhw[96:128, :], 0.5, "m_lw1")

    def table(ap, x, k, b, name):
        fin(S.activation(ap, x, F.Copy, bias=b, scale=k), name)

    need("s", "i_u")
    table(T.one[:], T.cu[:, 0:128], 0.0, 1.0, "a_one")
    for c in (0, 16):
        table(T.dfw[0:32, c:c + 16], T.cu[0:32, 16:32], -2.0, 29.0, "a_d")
    table(T.dfw[32:64, :], T.cu[32:64, 0:32], 0.0, 1.0, "a_d")
    table(T.dfw[64:128, :], T.cu[64:128, 0:32], 0.0, 0.0, "a_d")
    table(T.ccol[:], T.cu[:, 0:1], 0.0, 8.0, "a_d")
    need("s", "a_d")
    for c, p0, p1, x in ((15, 0, 32, -225.0), (15, 32, 64, -15.0), (15, 64, 128, 1.0), (31, 0, 64, 0.0)):
        table(T.dfw[p0:p1, c:c + 1], T.cu[p0:p1, 0:1], 0.0, x, "a_d1")
    table(T.ccol[0:32, :], T.cu[0:32, 0:1], 0.0, 64.0, "a_d1")
    need("g", "a_one")
    fin(g.affine_select(T.em0[:], T.one[:], [[0, 16], [-16, 8]], A.is_ge, 0.0, 0, 1), "i_e0")
    need("g", "i_e0")
    fin(g.affine_select(T.em[:], T.em0[:], [[0, 16], [16, 8]], A.is_ge, 0.0, 15, -1), "i_em")

    need("v", "s_pos")
    fin(V.tensor_copy(T.posb[:], T.posi[:]), "v_posb")
    fin(V.tensor_copy(T.posf[:], T.posi[:]), "v_posf")
    need("t", "v_sel", "v_posb")
    fin(E.matmul(T.pm[:, 0:2], T.sel8[:], T.posb[:], True, True), "t_pos")
    need("s", "t_pos")
    fin(S.activation(T.neg[:], T.pm[:, 0:2], F.Copy, scale=-1.0), "a_neg")
    need("s", "a_neg", "i_aj", "i_bj", "v_cmid", "v_col")
    for h in range(2):
        c = slice(128 * h, 128 * h + 128)
        fin(S.activation(T["pf%d" % h][:, 0:128], T.aj[:, c], F.Square, bias=T.neg[:, 0:1]), "a_xx%d" % h)
        fin(S.activation(T.yy[:, c], T.bj[:, c], F.Square, bias=T.neg[:, 1:2]), "a_xx%d" % h)
        if h == 0:
            fin(S.activation(T.dyc[:], T.bj[:, 0:256:16], F.Square, bias=T.neg[:, 1:2]), "a_dc")
            fin(S.activation(T.dxc[:], T.cmid[:], F.Square, bias=T.neg[:, 0:1]), "a_dc")
    fin(S.activation(T.rx2[:], T.cols[:, 1:2], F.Square, bias=T.neg[:, 0:1]), "a_rx")
    for h in range(2):
        c = slice(128 * h, 128 * h + 128)
        need("v", "a_xx%d" % h)
        fin(V.tensor_tensor(T.ss[:, c], T["pf%d" % h][:, 0:128], T.yy[:, c], A.add), "v_ss%d" % h)
        if h == 0:
            need("v", "a_dc")
            fin(V.tensor_scalar(T.sl[:], T.dyc[:], T.dxc[:, 0:1], None, A.add), "v_sl")
            need("v", "v_sl")
            fin(V.tensor_scalar(T.ci[:], T.sl[:], 4, 511, A.arith_shift_right, A.bitwise_and), "v_ci")
            need("v", "v_ci")
            fin(V.tensor_copy(T.cidx[:], T.ci[:]), "v_cidx")
    for h in range(2):
        c = slice(128 * h, 128 * h + 128)
        need("s", "v_ss%d" % h, "v_wcol")
        fin(S.activation(T.rj[:, c], T.ss[:, c], F.Square, bias=T.wcol[:, 0:1], scale=1.0 / 4096), "a_t%d" % h)
    for h in range(2):
        c = slice(128 * h, 128 * h + 128)
        need("s", "a_t%d" % h)
        fin(S.activation(T.mask[:, c], T.rj[:, c], F.Relu, bias=1e7, scale=-1e7), "a_m")
    need("s", "a_rx")
    fin(S.activation(T.rxo[:], T.rx2[:], F.Copy, bias=-15.0 / 32, scale=0.0625), "a_rxo")

    def turn(cb):
        need("v", "s_tau")
        for i in (cb, cb + 1):
            fin(V.tensor_copy(T.pf[:, i, :, :], T.pin[:, :, 16 * i:16 * i + 16]), "v_pf%d" % cb)
        need("t", "v_pf%d" % cb, "v_idh")
        for i in (cb, cb + 1):
            ins = E.matmul(T.pe[:, i::4], T.pf[:, i, :, :], T.idh[:], True, True)
        if cb == 2:
            fin(ins, "t_n")

    turn(0)
    turn(2)
    need("v", "v_cidx", "a_m", "s_row")
    fin(V.tensor_tensor(T.yg[:], T.row[:, 0:512].indirect(T.cidx[:, 0:16]), T.mask[:], A.min), "v_yg")
    need("t", "v_yg", "v_bs")
    for r in range(16):
        ins = E.matmul(T.po[0:16, r:128:16], T.yg[:, r::16], T.bsel[:], True, True)
    fin(ins, "t_o1")
    need("v", "t_n")
    fin(V.tensor_copy(T.off[:, 0:256], T.pe[:, 0:256]), "v_off0")
    need("v", "t_o1")
    fin(V.tensor_copy(T.cgt[:], T.po[0:16, 0:128]), "v_cgt")
    need("t", "v_cgt", "v_idh")
    fin(E.matmul(T.pt[:, 0:16], T.cgt[:], T.idh[0:16, 0:16], True, True), "t_off")
    fin(V.tensor_copy(T.off[:, 256:512], T.pe[:, 256:512]), "v_off1")
    need("v", "t_off")
    fin(V.tensor_copy(T.off2[:], T.pt[:, 0:16]), "v_off2")
    need("v", "v_off2", "s_tr")
    fin(V.tensor_copy(T.cg[:], T.trs[:, 0:2048].indirect(T.off2[:])), "v_cg")
    need("t", "v_qs", "v_cg")
    for b in range(4):
        for h in range(2):
            c = 128 * h + 32 * b
            ins = E.matmul(T.pc[32 * b:32 * b + 32, 0:32], T.qs[:, 16 - 16 * h:48 - 16 * h], T.cg[:, c:c + 32], h == 0, h == 1)
    fin(ins, "t_c")

    def zs(a, b):
        need("s", "v_off0", "s_tr")
        if b > 256:
            need("s", "v_off1")
        fin(S.activation(T.zed[:, 16 * a:16 * b], T.trs[:, 0:2048].indirect(T.off[:, a:b]), F.Copy), "a_z")

    def zv(a, b):
        need("v", "v_off0", "v_off1", "s_tr")
        fin(V.tensor_copy(T.zed[:, 16 * a:16 * b], T.trs[:, 0:2048].indirect(T.off[:, a:b])), "v_z")

    zv(Z3, ZG)
    need("v", "t_c")
    fin(V.tensor_copy(T.sendc[:], T.pc[:, 0:32]), "v_sendc")
    need("v", "v_posf", "m_ft")
    fin(V.tensor_scalar(T.feat[:, 32:64], T.feat[:, 0:32], T.posf[:, 0:1], -1.0, A.mult, A.mult), "v_feat")
    fin(V.tensor_scalar(T.feat[:, 96:128], T.feat[:, 0:32], T.posf[:, 1:2], -1.0, A.mult, A.mult), "v_feat")
    mine = slice(32 * rank, 32 * rank + 32)
    rc = T.sem["r_c%d" % rank]
    tr = [RemoteDMATransfer(dst_ids=[dst(d) for d in off], dma_engine_mask=bits(oe), remote_sem=rc,
                            srcs=[T.sendc[:]], dsts=[T.landc[:, mine] for d in off])]
    if on:
        tr.append(RemoteDMATransfer(dst_ids=[dst(d) for d in on], dma_engine_mask=bits(ne), remote_sem=rc,
                                    srcs=[T.sendc[:]], dsts=[T.landc[:, mine] for d in on]))
    need("g", "v_sendc")
    g.remote_dma_fused(tr, local_sem=T.sem["l_c"])
    cnt["l_c"] = len(oe) + (len(ne) if on else 0)
    for r in others(rank):
        o, e1, o2, e2 = coarse_masks(r)
        cnt["r_c%d" % r] = len(e1) if rank in o else len(e2)
    iota(T.coef[:], [[32 * half * (h1 - h0), 2], [32, half], [1, 16]], 8 + 32 * half * h0, 0, "i_c")
    fin(g.affine_select(T.idf[:], T.one[:], [[-1, 128]], A.is_equal, 0.0, 0, 1), "i_id")
    iota(T.kw[:], [[32, 8]], 0, 0, "i_kw")

    zs(0, Z1)
    need("t", "v_feat", "m_ft", "m_tr1", "i_rr", "a_neg")
    E.matmul(T.pm[:, 128:256], T.feat[:], T.sel8[:], True, False)
    fin(E.matmul(T.pm[:, 128:256], T.trow[:], T.rrow[:], False, True), "t_lh4")
    need("s", "t_lh4")
    fin(S.activation(T.lh4[:], T.pm[:, 128:256], F.Copy), "a_lh4")
    need("s", "i_ky", "r_t")
    fin(S.activation(T.kysq[:], T.kyi[:], F.Square, bias=T.neg[:, 1:2]), "a_ky")
    zs(Z1, Z2)
    zv(ZG, ZV)
    need("v", "i_k", "r_t", "a_d1")
    fin(V.tensor_scalar(T.gee[:], T.kcol[:], T.cols[:, 2:3], T.ccol[:, 0:1], A.is_equal, A.mult), "v_km")
    need("v", "v_km", "i_c")
    fin(V.tensor_tensor(T.gee[64:96, :], T.gee[64:96, :], T.coef[64:96, :], A.mult), "v_g")
    zv(ZV, ZC)

    need("t", "v_off0", "v_off1", "v_sendc")
    E.matmul(T.pe[:, 0:32], T.idh[:], T.sendc[:], True, False)
    for i, r in enumerate([r for r in others(rank) if r in on] + [r for r in others(rank) if r not in on]):
        need("t", "r_c%d" % r)
        ins = E.matmul(T.pe[:, 0:32], T.idh[:], T.landc[:, 32 * r:32 * r + 32], False, i == n - 2)
    fin(ins, "t_sum")
    need("s", "t_sum")
    fin(S.activation(T.sq[:], T.pe[:, 0:32], F.Square), "a_sq")
    need("t", "a_sq", "i_em")
    zs(Z2, Z3)
    fin(E.matmul(T.pe[:, 64:96], T.em[:], T.sq[:], True, True), "t_e")
    need("t", "i_id", "a_ky")
    E.matmul(T.ps[:, 0:128], T.idf[:], T.kysq[:], True, False)
    need("v", "t_e")
    fin(V.tensor_reduce(T.mx[:], T.pe[:, 64:96], AxisListType.X, A.max), "v_mx")
    need("v", "v_mx")
    fin(V.tensor_scalar(T.uu[:], T.pe[:, 64:96], T.mx[:, 0:1], None, A.is_lt), "v_u")
    need("v", "v_u", "a_d1")
    fin(V.tensor_tensor_scan(T.ff[:], T.uu[:], T.dfw[:], 0.0, A.mult, A.add), "v_f")
    need("v", "v_f", "v_g")
    fin(V.tensor_scalar(T.rhs[:], T.gee[:], T.ff[:, 31:32], None, A.mult), "v_rhs")
    need("t", "v_rhs", "a_lh4")
    fin(E.matmul(T.ps[:, 0:128], T.lh4[:], T.rhs[:], False, True), "t_s")
    need("t", "m_lw1")
    for k0, c in hs:
        fin(E.matmul(T.pm[0:1, 300 + k0:304 + k0], T.lhw[:], T.rhs[:, c.start:c.stop:16], True, True), "t_w")
    need("v", "t_s", "a_rxo")
    for h, (k0, c) in enumerate(hs):
        fin(V.tensor_scalar(T.lst[:, c], T.ps[:, c], 0.0625, T.rxo[:, 0:1], A.mult, A.add), "v_l%d" % h)

    need("v", "v_z", "a_z")
    need("s", "v_z", "a_z")

    def pick(q, i):
        o = T.fg[:, 256 * i:256 * i + 256]
        w = T.zed[:, 0:ZL].indirect(T.lst[:, 16 * i:16 * i + 16])
        need(q, "v_l%d" % (i // half))
        if q == "s":
            fin(S.activation(o, w, F.Copy), "p%d" % i)
        else:
            fin(V.tensor_copy(o, w), "p%d" % i)

    def add_up(h):
        for i in [half * h + x for x in (2, 0, 3, 1)]:
            need("t", "p%d" % i)
            for u in range(2):
                c = 32 * (i - half * h) + u
                ins = E.matmul(T["pf%d" % h][:, c:c + 31:2], T.fg[:, 256 * i + 128 * u:256 * i + 128 * u + 128],
                               T.qs[:, 16:32], True, True)
        fin(ins, "t_f%d" % h)

    def ready(h):
        need("v", "t_f%d" % h)
        fin(V.tensor_copy(T.sendf[:, 128 * h:128 * h + 128], T["pf%d" % h][:, 0:128]), "v_e%d" % h)

    for i in (0, 1, 4, 5):
        pick("s", i)
    for i in (2, 3):
        pick("v", i)
    add_up(0)
    pick("v", 6)
    ready(0)
    pick("v", 7)
    add_up(1)
    ready(1)

    for h in range(2):
        dests = sorted(halves(rank)[h], key=lambda d: far(rank, d))
        em = masks(rank, dests)
        need("g", "v_e%d" % h)
        tr = []
        for d in dests:
            k = korder.index(d)
            tr.append(RemoteDMATransfer(dst_ids=[dst(d)], dma_engine_mask=bits(em[d]), remote_sem=T.sem["r_f%d" % rank],
                                        srcs=[T.sendf[:, 32 * k:32 * k + 32]], dsts=[T.landf[:, mine]]))
            cnt["l_f"] = cnt.get("l_f", 0) + len(em[d])
        g.remote_dma_fused(tr, local_sem=T.sem["l_f"])
    early = [r for r in others(rank) if rank in halves(r)[0]]
    late = [r for r in others(rank) if rank in halves(r)[1]]
    late = [r for r in late if r in on] + [r for r in late if r not in on]
    for h, rs in enumerate([early, late]):
        for r in rs:
            cnt["r_f%d" % r] = len(masks(r, halves(r)[h])[rank])

    need("v", "t_w", "i_kw")
    fin(V.tensor_tensor(T.wout[:], T.pm[0:1, 300:308], T.kw[:], A.add), "v_w")
    need("y", "v_w")
    fin(Y.dma_start(T.w[:], T.wout[:]), "s_w", 16)

    need("t", "v_e1")
    k = korder.index(rank)
    E.matmul(T.pc[0:32, 0:128], T.sendf[:, 32 * k:32 * k + 32], T.idh[:], True, False)
    for i, r in enumerate(early + late):
        need("t", "r_f%d" % r)
        ins = E.matmul(T.pc[0:32, 0:128], T.landf[:, 32 * r:32 * r + 32], T.idh[:], False, i == n - 2)
    fin(ins, "t_y")
    need("v", "t_y")
    fin(V.tensor_copy(T.yout[:], T.pc[0:32, 0:128]), "v_y")
    need("y", "v_y")
    fin(Y.dma_start(T.y[:], T.yout[:]), "s_y", 16)
    need("y", "s_w", "s_y")
    done = {}
    for (q, nm), k in seen.items():
        done[nm] = max(done.get(nm, 0), k)
    for nm in list(cnt):
        if done.get(nm, 0) < cnt[nm]:
            need("g", nm)
